import numpy as np
import ml_dtypes


def mxq(x, axis, fmt="e4m3"):
    dtype, down = {"e4m3": (ml_dtypes.float8_e4m3fn, 7), "e5m2": (ml_dtypes.float8_e5m2, 14)}[fmt]
    v = np.moveaxis(np.asarray(x, np.float32).astype(ml_dtypes.bfloat16).astype(np.float64), axis, -1)
    blocks = v.reshape(v.shape[:-1] + (-1, 32))
    amax = np.abs(blocks).max(-1, keepdims=True)
    byte = np.maximum(np.where(amax > 0, np.frexp(amax)[1] - 1 + 127, 0) - down, 1)
    scale = np.exp2(byte - 127.0)
    codes = (blocks / scale).astype(np.float32).astype(dtype).astype(np.float64)
    return np.moveaxis((codes * scale).reshape(v.shape), -1, axis)


WIDE = False


def mx_kscale(k):
    if not WIDE:
        return np.ones(k)
    levels = np.array([10, -10, 5, -5, 0])
    if k % 512:
        return np.exp2(np.random.permutation(np.resize(levels, k // 32))).repeat(32)
    a = np.empty((k // 512, 16))
    for p in range(k // 512):
        a[p, :8] = np.random.permutation(np.resize(levels, 8))
        for g in range(8):
            far = levels[np.abs(levels - a[p, g]) >= 10]
            a[p, g + 8] = far[np.random.randint(len(far))]
    return np.exp2(a.ravel()).repeat(32)


def f64(x):
    return np.asarray(x).astype(np.float64)


def striped(idx):
    return np.tile(idx.reshape(-1, 16).T, (8, 1)).astype(np.uint16)


def unstriped(offs):
    return offs[:16].T.reshape(-1).astype(np.int64)


def pack_weight(w):
    k, n = w.shape
    w = f64(np.asarray(w, np.float32).astype(ml_dtypes.bfloat16)).reshape(k // 32, 32, n)
    amax = np.abs(w).max(1)
    byte = np.clip(np.where(amax > 0, np.frexp(amax)[1] - 1 + 127 - 7, 1), 1, 254)
    scaled = (w * np.exp2(127.0 - byte)[:, None, :]).reshape(k, n).astype(np.float32)
    words = np.ascontiguousarray(scaled.reshape(k // 512, 128, 4, n).transpose(0, 1, 3, 2)).astype(ml_dtypes.float8_e4m3fn).view(np.uint8)
    return words, np.ascontiguousarray(byte.astype(np.uint8).reshape(k // 512, 16, n))


def unpack_weight(words, scales):
    g, p, n, _ = words.shape
    vals = np.ascontiguousarray(words).view(ml_dtypes.float8_e4m3fn).astype(np.float64) * np.repeat(np.exp2(scales.astype(np.float64) - 127.0), 8, axis=1)[..., None]
    return vals.transpose(0, 1, 3, 2).reshape(g * 512, n)


def gelu(v):
    return 0.5 * v * (1.0 + np.tanh(np.sqrt(2.0 / np.pi) * (v + 0.044715 * v**3)))


K, T, S, H, N = 1024, 2048, 512, 512, 256


def setup_inputs():
    n = np.random.standard_normal
    s = mx_kscale(K)[:, None]
    u = mx_kscale(H)
    packed_xT = pack_weight(n((K, T)) * s)
    packed_w2 = pack_weight(n((H, N)) / np.sqrt(H) / u[:, None])
    return {
        "x_words": packed_xT[0],
        "x_scales": packed_xT[1],
        "w1": (n((K, H)) / np.sqrt(K) / s * u).astype(np.float32),
        "w2_words": packed_w2[0],
        "w2_scales": packed_w2[1],
        "pe": (0.5 * n((H, T)) * u[:, None]).astype(np.float32),
        "offs": striped(np.random.permutation(T)[:S]),
    }


def reference(x_words, x_scales, w1, w2_words, w2_scales, pe, offs):
    xq = unpack_weight(x_words, x_scales)[:, unstriped(offs)]
    g = f64(pe)[:, unstriped(offs)]
    h = gelu((mxq(f64(w1), 0, "e4m3").T @ xq) + g)
    return unpack_weight(w2_words, w2_scales).T @ mxq(h, 0, "e4m3")

@@ -1,0 +1,164 @@
+from contextlib import ExitStack
+
+import concourse.mybir as mybir
+
+K, T, S, H, N = 1024, 2048, 512, 512, 256
+FLOPS = 2 * K * H * S + 2 * H * N * S
+
+F32 = mybir.dt.float32
+BF16 = mybir.dt.bfloat16
+I32 = mybir.dt.int32
+U32 = mybir.dt.uint32
+U16 = mybir.dt.uint16
+U8 = mybir.dt.uint8
+FP8X4 = mybir.dt.float8_e4m3fn_x4
+ADD = mybir.AluOpType.add
+GELU = mybir.ActivationFunctionType.Gelu_apprx_tanh
+
+P = 128
+PACK = 4
+K_PASS = P * PACK
+PASSES = K // K_PASS
+QUADS = 4
+HALF = S // 2
+PIECE = 128
+PIECES = S // PIECE
+LIST_ROWS = 16
+
+
+def tile_picked_posadd_gelu_p_kernel(
+    tc, x_words, x_scales, w1, w2_words, w2_scales, pe, offs, out
+):
+    nc = tc.nc
+    with ExitStack() as ctx:
+        keep = ctx.enter_context(tc.tile_pool(name="keep", bufs=1))
+        psum = ctx.enter_context(tc.psum_pool(name="psum", bufs=1))
+
+        w1_raw = [keep.tile([P, PACK, H], F32, name=f"w1_raw{z}") for z in range(PASSES)]
+        x_table = [keep.tile([P, T], I32, name=f"x_table{z}") for z in range(PASSES)]
+        pe_table = [keep.tile([P, T], F32, name=f"pe_table{t}") for t in range(PACK)]
+        offsets = keep.tile([P, S // LIST_ROWS], U16, name="offsets")
+        xs_table = keep.tile([P, T], U8, name="xs_table")
+        w2_codes = keep.tile([P, N], I32, name="w2_codes", align_bytes=64)
+        w2_plane = keep.tile([P, N], U8, name="w2_plane", align_bytes=64)
+
+        nc.vector.memset(xs_table[:].bitcast(I32), 0)
+        nc.vector.memset(w2_plane[:].bitcast(I32), 0)
+
+        for z in range(PASSES):
+            rows = w1[z * K_PASS : (z + 1) * K_PASS, :]
+            nc.sync.dma_start(out=w1_raw[z][:], in_=rows.rearrange("(p j) c -> p j c", j=PACK))
+        nc.sync.dma_start(offsets[:], offs)
+        for q in range(QUADS):
+            nc.sync.dma_start(
+                out=xs_table[32 * q : 32 * q + 4 * PASSES, :].bitcast(I32),
+                in_=x_scales[:, 4 * q : 4 * q + 4, :].bitcast(I32),
+            )
+        for z in range(PASSES):
+            nc.sync.dma_start(out=x_table[z][:], in_=x_words[z].rearrange("p n r -> p (n r)").bitcast(I32))
+        pe_rows = pe.rearrange("(p t) c -> p t c", t=PACK)
+        for t in range(PACK):
+            nc.sync.dma_start(out=pe_table[t][:], in_=pe_rows[:, t, :])
+        nc.sync.dma_start(out=w2_codes[:], in_=w2_words[0].rearrange("p n r -> p (n r)").bitcast(I32))
+
+        for q in range(QUADS):
+            nc.sync.dma_start(
+                out=w2_plane[32 * q : 32 * q + 4, :].bitcast(I32),
+                in_=w2_scales[0, 4 * q : 4 * q + 4, :].bitcast(I32),
+            )
+
+        w1_codes, w1_plane = [], []
+        for z in range(PASSES):
+            grouped = keep.tile([P, PACK * H], BF16, name=f"w1_grouped{z}", align_bytes=64)
+            nc.scalar.copy(
+                out=grouped[:].rearrange("p (t m j) -> p m j t", t=PACK, j=PACK),
+                in_=w1_raw[z][:].rearrange("p j (m t) -> p m j t", t=PACK),
+            )
+            codes = keep.tile([P, H], U32, name=f"w1_codes{z}", align_bytes=64)
+            plane = keep.tile([P, H], U8, name=f"w1_plane{z}", align_bytes=64)
+            nc.vector.quantize_mx(out=codes[:].bitcast(FP8X4), scales=plane[:], in_=grouped[:])
+            w1_codes.append(codes)
+            w1_plane.append(plane)
+
+        x_codes = []
+        for z in range(PASSES):
+            picked = keep.tile([P, S], U32, name=f"x_codes{z}", align_bytes=64)
+            nc.vector.tensor_copy(picked[:], x_table[z][:].bitcast(U32).indirect(offsets[:]))
+            x_codes.append(picked)
+        x_planes = keep.tile([P, S], U8, name="x_planes", align_bytes=64)
+        nc.vector.tensor_copy(x_planes[:], xs_table[:].indirect(offsets[:]))
+
+        acc = [psum.tile([P, S], F32, name=f"acc{t}") for t in range(PACK)]
+        for z in range(PASSES):
+            for t in range(PACK):
+                cols = slice(t * P, (t + 1) * P)
+                nc.tensor.matmul_mx(
+                    out=acc[t][:],
+                    lhsT=w1_codes[z][:, cols].bitcast(FP8X4),
+                    lhsT_scale=w1_plane[z][:, cols],
+                    rhs=x_codes[z][:].bitcast(FP8X4),
+                    rhs_scale=x_planes[4 * z : P, :],
+                    start=(z == 0),
+                    stop=(z == PASSES - 1),
+                )
+
+        hidden = [keep.tile([P, PIECE, PACK], BF16, name=f"hidden{c}", align_bytes=64) for c in range(PIECES)]
+
+        def look_up(t, j0, width):
+            picked = keep.tile([P, width], F32, name=f"pe_picked{t}_{j0}")
+            entries = offsets[:, j0 // LIST_ROWS : (j0 + width) // LIST_ROWS]
+            nc.vector.tensor_copy(picked[:], pe_table[t][:].indirect(entries))
+            return picked
+
+        early = keep.tile([P, 2, S], F32, name="early")
+        for t in range(2):
+            picked = look_up(t, 0, S)
+            nc.vector.tensor_tensor(early[:, t, :], acc[t][:], picked[:], ADD)
+        for c in range(PIECES):
+            cols = slice(c * PIECE, (c + 1) * PIECE)
+            nc.scalar.activation(hidden[c][:, :, 0:2], early[:, :, cols].rearrange("p t j -> p j t"), GELU)
+
+        t = 2
+        for j0 in range(0, S, HALF):
+            picked = look_up(t, j0, HALF)
+            summed = keep.tile([P, HALF], F32, name=f"summed{t}_{j0}")
+            nc.vector.tensor_tensor(summed[:], acc[t][:, j0 : j0 + HALF], picked[:], ADD)
+            for c0 in range(0, HALF, PIECE):
+                nc.scalar.activation(hidden[(j0 + c0) // PIECE][:, :, t], summed[:, c0 : c0 + PIECE], GELU)
+
+        t = 3
+        out_rows = out.rearrange("(u p) j -> p u j", p=P)
+        for j0 in range(0, S, HALF):
+            picked = look_up(t, j0, HALF)
+            for c0 in range(0, HALF, PIECE):
+                c = (j0 + c0) // PIECE
+                cols = slice(c * PIECE, (c + 1) * PIECE)
+                summed = keep.tile([P, PIECE], F32, name=f"summed{t}_{c}")
+                nc.vector.tensor_tensor(summed[:], acc[t][:, cols], picked[:, c0 : c0 + PIECE], ADD)
+                nc.scalar.activation(hidden[c][:, :, t], summed[:], GELU)
+
+        for c in range(PIECES):
+            cols = slice(c * PIECE, (c + 1) * PIECE)
+            h_codes = keep.tile([P, PIECE], U32, name=f"h_codes{c}", align_bytes=64)
+            h_plane = keep.tile([P, PIECE], U8, name=f"h_plane{c}", align_bytes=64)
+            nc.vector.quantize_mx(
+                out=h_codes[:].bitcast(FP8X4), scales=h_plane[:], in_=hidden[c][:].rearrange("p j t -> p (j t)")
+            )
+            product = psum.tile([P, N // P, PIECE], F32, name=f"product{c}")
+            for u in range(N // P):
+                rows = slice(u * P, (u + 1) * P)
+                nc.tensor.matmul_mx(
+                    out=product[:, u, :],
+                    lhsT=w2_codes[:, rows].bitcast(FP8X4),
+                    lhsT_scale=w2_plane[:, rows],
+                    rhs=h_codes[:].bitcast(FP8X4),
+                    rhs_scale=h_plane[:],
+                    start=True,
+                    stop=True,
+                )
+            result = keep.tile([P, N // P, PIECE], F32, name=f"result{c}")
+            if c % 2 == 0:
+                nc.vector.tensor_copy(result[:], product[:])
+            else:
+                nc.scalar.copy(result[:], product[:])
+            nc.sync.dma_start(out=out_rows[:, :, cols], in_=result[:])

@@ -32,6 +32,7 @@ def tile_picked_posadd_gelu_p_kernel(
     nc = tc.nc
     with ExitStack() as ctx:
         keep = ctx.enter_context(tc.tile_pool(name="keep", bufs=1))
+        ring = ctx.enter_context(tc.tile_pool(name="ring", bufs=3))
         psum = ctx.enter_context(tc.psum_pool(name="psum", bufs=1))
 
         w1_raw = [keep.tile([P, PACK, H], F32, name=f"w1_raw{z}") for z in range(PASSES)]
@@ -88,7 +89,7 @@ def tile_picked_posadd_gelu_p_kernel(
         x_planes = keep.tile([P, S], U8, name="x_planes", align_bytes=64)
         nc.vector.tensor_copy(x_planes[:], xs_table[:].indirect(offsets[:]))
 
-        acc = [psum.tile([P, S], F32, name=f"acc{t}") for t in range(PACK)]
+        acc = [psum.tile([P, S], F32, name=f"acc{t}", tag=f"acc{t}") for t in range(PACK)]
         for z in range(PASSES):
             for t in range(PACK):
                 cols = slice(t * P, (t + 1) * P)
@@ -110,45 +111,39 @@ def tile_picked_posadd_gelu_p_kernel(
             nc.vector.tensor_copy(picked[:], pe_table[t][:].indirect(entries))
             return picked
 
-        early = keep.tile([P, 2, S], F32, name="early")
-        for t in range(2):
-            picked = look_up(t, 0, S)
-            nc.vector.tensor_tensor(early[:, t, :], acc[t][:], picked[:], ADD)
-        for c in range(PIECES):
-            cols = slice(c * PIECE, (c + 1) * PIECE)
-            nc.scalar.activation(hidden[c][:, :, 0:2], early[:, :, cols].rearrange("p t j -> p j t"), GELU)
+        for t in range(PACK):
+            gather_width, add_width = (S, HALF) if t < 2 else (HALF, PIECE)
+            for j0 in range(0, S, gather_width):
+                picked = look_up(t, j0, gather_width)
+                for a0 in range(0, gather_width, add_width):
+                    summed = keep.tile([P, add_width], F32, name=f"summed{t}_{j0 + a0}")
+                    nc.vector.tensor_tensor(
+                        summed[:], acc[t][:, j0 + a0 : j0 + a0 + add_width], picked[:, a0 : a0 + add_width], ADD
+                    )
+                    for c0 in range(0, add_width, PIECE):
+                        piece = hidden[(j0 + a0 + c0) // PIECE]
+                        nc.scalar.activation(piece[:, :, t], summed[:, c0 : c0 + PIECE], GELU)
 
-        t = 2
-        for j0 in range(0, S, HALF):
-            picked = look_up(t, j0, HALF)
-            summed = keep.tile([P, HALF], F32, name=f"summed{t}_{j0}")
-            nc.vector.tensor_tensor(summed[:], acc[t][:, j0 : j0 + HALF], picked[:], ADD)
-            for c0 in range(0, HALF, PIECE):
-                nc.scalar.activation(hidden[(j0 + c0) // PIECE][:, :, t], summed[:, c0 : c0 + PIECE], GELU)
-
-        t = 3
         out_rows = out.rearrange("(u p) j -> p u j", p=P)
-        for j0 in range(0, S, HALF):
-            picked = look_up(t, j0, HALF)
-            for c0 in range(0, HALF, PIECE):
-                c = (j0 + c0) // PIECE
-                cols = slice(c * PIECE, (c + 1) * PIECE)
-                summed = keep.tile([P, PIECE], F32, name=f"summed{t}_{c}")
-                nc.vector.tensor_tensor(summed[:], acc[t][:, cols], picked[:, c0 : c0 + PIECE], ADD)
-                nc.scalar.activation(hidden[c][:, :, t], summed[:], GELU)
-
         for c in range(PIECES):
             cols = slice(c * PIECE, (c + 1) * PIECE)
-            h_codes = keep.tile([P, PIECE], U32, name=f"h_codes{c}", align_bytes=64)
-            h_plane = keep.tile([P, PIECE], U8, name=f"h_plane{c}", align_bytes=64)
+            h_codes = ring.tile([P, PIECE], U32, name="h_codes", align_bytes=64)
+            h_plane = ring.tile([P, PIECE], U8, name="h_plane", align_bytes=64)
             nc.vector.quantize_mx(
                 out=h_codes[:].bitcast(FP8X4), scales=h_plane[:], in_=hidden[c][:].rearrange("p j t -> p (j t)")
             )
-            product = psum.tile([P, N // P, PIECE], F32, name=f"product{c}")
+            last = c == PIECES - 1
+            result = keep.tile([P, N // P, PIECE], F32, name=f"result{c}")
+            if last:
+                banks = [psum.tile([P, PIECE], F32, name=f"product{c}"), psum.tile([P, PIECE], F32, name="tail", tag="acc0")]
+                products = [bank[:] for bank in banks]
+            else:
+                bank = psum.tile([P, N // P, PIECE], F32, name=f"product{c}")
+                products = [bank[:, u, :] for u in range(N // P)]
             for u in range(N // P):
                 rows = slice(u * P, (u + 1) * P)
                 nc.tensor.matmul_mx(
-                    out=product[:, u, :],
+                    out=products[u],
                     lhsT=w2_codes[:, rows].bitcast(FP8X4),
                     lhsT_scale=w2_plane[:, rows],
                     rhs=h_codes[:].bitcast(FP8X4),
@@ -156,9 +151,11 @@ def tile_picked_posadd_gelu_p_kernel(
                     start=True,
                     stop=True,
                 )
-            result = keep.tile([P, N // P, PIECE], F32, name=f"result{c}")
-            if c % 2 == 0:
-                nc.vector.tensor_copy(result[:], product[:])
+            if last:
+                for u in range(N // P):
+                    nc.vector.tensor_copy(result[:, u, :], products[u])
+            elif c == 0:
+                nc.vector.tensor_copy(result[:], bank[:])
             else:
-                nc.scalar.copy(result[:], product[:])
+                nc.scalar.copy(result[:], bank[:])
             nc.sync.dma_start(out=out_rows[:, :, cols], in_=result[:])

@@ -32,7 +32,6 @@ def tile_picked_posadd_gelu_p_kernel(
     nc = tc.nc
     with ExitStack() as ctx:
         keep = ctx.enter_context(tc.tile_pool(name="keep", bufs=1))
-        ring = ctx.enter_context(tc.tile_pool(name="ring", bufs=3))
         psum = ctx.enter_context(tc.psum_pool(name="psum", bufs=1))
 
         w1_raw = [keep.tile([P, PACK, H], F32, name=f"w1_raw{z}") for z in range(PASSES)]
@@ -48,7 +47,10 @@ def tile_picked_posadd_gelu_p_kernel(
 
         for z in range(PASSES):
             rows = w1[z * K_PASS : (z + 1) * K_PASS, :]
-            nc.sync.dma_start(out=w1_raw[z][:], in_=rows.rearrange("(p j) c -> p j c", j=PACK))
+            for j in range(0, PACK, 2):
+                nc.sync.dma_start(
+                    out=w1_raw[z][:, j : j + 2, :], in_=rows.rearrange("(p j) c -> p j c", j=PACK)[:, j : j + 2, :]
+                )
         nc.sync.dma_start(offsets[:], offs)
         for q in range(QUADS):
             nc.sync.dma_start(
@@ -68,10 +70,18 @@ def tile_picked_posadd_gelu_p_kernel(
                 in_=w2_scales[0, 4 * q : 4 * q + 4, :].bitcast(I32),
             )
 
+        warm = keep.tile([P, 8], F32, name="warm")
+        nc.vector.memset(warm[:, 0:4], 0.0)
+        nc.scalar.activation(warm[:, 4:8], warm[:, 0:4], GELU)
+
+        x_planes = keep.tile([P, S], U8, name="x_planes", align_bytes=64)
+        nc.vector.tensor_copy(x_planes[:], xs_table[:].indirect(offsets[:]))
+
         w1_codes, w1_plane = [], []
         for z in range(PASSES):
             grouped = keep.tile([P, PACK * H], BF16, name=f"w1_grouped{z}", align_bytes=64)
-            nc.scalar.copy(
+            copy = nc.scalar.copy if z == 0 else nc.vector.tensor_copy
+            copy(
                 out=grouped[:].rearrange("p (t m j) -> p m j t", t=PACK, j=PACK),
                 in_=w1_raw[z][:].rearrange("p j (m t) -> p m j t", t=PACK),
             )
@@ -86,8 +96,6 @@ def tile_picked_posadd_gelu_p_kernel(
             picked = keep.tile([P, S], U32, name=f"x_codes{z}", align_bytes=64)
             nc.vector.tensor_copy(picked[:], x_table[z][:].bitcast(U32).indirect(offsets[:]))
             x_codes.append(picked)
-        x_planes = keep.tile([P, S], U8, name="x_planes", align_bytes=64)
-        nc.vector.tensor_copy(x_planes[:], xs_table[:].indirect(offsets[:]))
 
         acc = [psum.tile([P, S], F32, name=f"acc{t}", tag=f"acc{t}") for t in range(PACK)]
         for z in range(PASSES):
@@ -102,33 +110,34 @@ def tile_picked_posadd_gelu_p_kernel(
                     start=(z == 0),
                     stop=(z == PASSES - 1),
                 )
+        first = [keep.tile([P, S], F32, name=f"first{t}") for t in range(PACK)]
+        for t in range(PACK):
+            nc.scalar.copy(first[t][:], acc[t][:])
 
         hidden = [keep.tile([P, PIECE, PACK], BF16, name=f"hidden{c}", align_bytes=64) for c in range(PIECES)]
 
-        def look_up(t, j0, width):
-            picked = keep.tile([P, width], F32, name=f"pe_picked{t}_{j0}")
+        def look_up(summed, t, j0, width):
             entries = offsets[:, j0 // LIST_ROWS : (j0 + width) // LIST_ROWS]
-            nc.vector.tensor_copy(picked[:], pe_table[t][:].indirect(entries))
-            return picked
+            nc.vector.tensor_tensor(summed, pe_table[t][:].indirect(entries), first[t][:, j0 : j0 + width], ADD)
 
-        for t in range(PACK):
-            gather_width, add_width = (S, HALF) if t < 2 else (HALF, PIECE)
-            for j0 in range(0, S, gather_width):
-                picked = look_up(t, j0, gather_width)
-                for a0 in range(0, gather_width, add_width):
-                    summed = keep.tile([P, add_width], F32, name=f"summed{t}_{j0 + a0}")
-                    nc.vector.tensor_tensor(
-                        summed[:], acc[t][:, j0 + a0 : j0 + a0 + add_width], picked[:, a0 : a0 + add_width], ADD
-                    )
-                    for c0 in range(0, add_width, PIECE):
-                        piece = hidden[(j0 + a0 + c0) // PIECE]
-                        nc.scalar.activation(piece[:, :, t], summed[:, c0 : c0 + PIECE], GELU)
+        early = keep.tile([P, 2, S], F32, name="early")
+        for t in range(2):
+            look_up(early[:, t, :], t, 0, S)
+        for c in range(PIECES):
+            cols = slice(c * PIECE, (c + 1) * PIECE)
+            nc.scalar.activation(hidden[c][:, :, 0:2], early[:, :, cols].rearrange("p t j -> p j t"), GELU)
+        late = [keep.tile([P, 2, PIECE], F32, name=f"late{c}") for c in range(PIECES)]
+        for c in range(PIECES):
+            look_up(late[c][:, 0, :], 2, c * PIECE, PIECE)
+        for c in range(PIECES):
+            look_up(late[c][:, 1, :], 3, c * PIECE, PIECE)
+            nc.scalar.activation(hidden[c][:, :, 2:4], late[c][:].rearrange("p t j -> p j t"), GELU)
 
         out_rows = out.rearrange("(u p) j -> p u j", p=P)
         for c in range(PIECES):
             cols = slice(c * PIECE, (c + 1) * PIECE)
-            h_codes = ring.tile([P, PIECE], U32, name="h_codes", align_bytes=64)
-            h_plane = ring.tile([P, PIECE], U8, name="h_plane", align_bytes=64)
+            h_codes = keep.tile([P, PIECE], U32, name=f"h_codes{c}", align_bytes=64)
+            h_plane = keep.tile([P, PIECE], U8, name=f"h_plane{c}", align_bytes=64)
             nc.vector.quantize_mx(
                 out=h_codes[:].bitcast(FP8X4), scales=h_plane[:], in_=hidden[c][:].rearrange("p j t -> p (j t)")
             )
@@ -152,10 +161,8 @@ def tile_picked_posadd_gelu_p_kernel(
                     stop=True,
                 )
             if last:
-                for u in range(N // P):
-                    nc.vector.tensor_copy(result[:, u, :], products[u])
-            elif c == 0:
-                nc.vector.tensor_copy(result[:], bank[:])
+                nc.vector.tensor_copy(result[:, 0, :], products[0])
+                nc.scalar.copy(result[:, 1, :], products[1])
             else:
                 nc.scalar.copy(result[:], bank[:])
             nc.sync.dma_start(out=out_rows[:, :, cols], in_=result[:])

@@ -20,10 +20,9 @@ PACK = 4
 K_PASS = P * PACK
 PASSES = K // K_PASS
 QUADS = 4
-HALF = S // 2
-PIECE = 128
-PIECES = S // PIECE
+QUAD = P // QUADS
 LIST_ROWS = 16
+WIDTHS = [128,128,128,128]
 
 
 def tile_picked_posadd_gelu_p_kernel(
@@ -34,54 +33,46 @@ def tile_picked_posadd_gelu_p_kernel(
         keep = ctx.enter_context(tc.tile_pool(name="keep", bufs=1))
         psum = ctx.enter_context(tc.psum_pool(name="psum", bufs=1))
 
-        w1_raw = [keep.tile([P, PACK, H], F32, name=f"w1_raw{z}") for z in range(PASSES)]
-        x_table = [keep.tile([P, T], I32, name=f"x_table{z}") for z in range(PASSES)]
-        pe_table = [keep.tile([P, T], F32, name=f"pe_table{t}") for t in range(PACK)]
         offsets = keep.tile([P, S // LIST_ROWS], U16, name="offsets")
-        xs_table = keep.tile([P, T], U8, name="xs_table")
-        w2_codes = keep.tile([P, N], I32, name="w2_codes", align_bytes=64)
-        w2_plane = keep.tile([P, N], U8, name="w2_plane", align_bytes=64)
+        nc.sync.dma_start(offsets[:], offs)
 
-        nc.vector.memset(xs_table[:].bitcast(I32), 0)
-        nc.vector.memset(w2_plane[:].bitcast(I32), 0)
+        xs_table = keep.tile([P, T], U8, name="xs_table", tag="slot_x1", align_bytes=64)
+        nc.vector.memset(xs_table[QUAD : 2 * QUAD, :].bitcast(I32), 0)
+        nc.vector.memset(xs_table[2 * QUAD : P, :].bitcast(I32), 0)
+        for z in range(PASSES):
+            nc.sync.dma_start(out=xs_table[z:QUAD:PASSES, :].bitcast(I32), in_=x_scales[z].bitcast(I32))
 
+        w1_raw = [keep.tile([P, PACK, H], F32, name=f"w1_raw{z}", tag=f"slot_pe{2 * z}", align_bytes=64) for z in range(PASSES)]
         for z in range(PASSES):
             rows = w1[z * K_PASS : (z + 1) * K_PASS, :]
-            for j in range(0, PACK, 2):
-                nc.sync.dma_start(
-                    out=w1_raw[z][:, j : j + 2, :], in_=rows.rearrange("(p j) c -> p j c", j=PACK)[:, j : j + 2, :]
-                )
-        nc.sync.dma_start(offsets[:], offs)
-        for q in range(QUADS):
-            nc.sync.dma_start(
-                out=xs_table[32 * q : 32 * q + 4 * PASSES, :].bitcast(I32),
-                in_=x_scales[:, 4 * q : 4 * q + 4, :].bitcast(I32),
-            )
-        for z in range(PASSES):
-            nc.sync.dma_start(out=x_table[z][:], in_=x_words[z].rearrange("p n r -> p (n r)").bitcast(I32))
-        pe_rows = pe.rearrange("(p t) c -> p t c", t=PACK)
-        for t in range(PACK):
-            nc.sync.dma_start(out=pe_table[t][:], in_=pe_rows[:, t, :])
-        nc.sync.dma_start(out=w2_codes[:], in_=w2_words[0].rearrange("p n r -> p (n r)").bitcast(I32))
+            nc.sync.dma_start(out=w1_raw[z][:], in_=rows.rearrange("(p j) c -> p j c", j=PACK))
 
-        for q in range(QUADS):
-            nc.sync.dma_start(
-                out=w2_plane[32 * q : 32 * q + 4, :].bitcast(I32),
-                in_=w2_scales[0, 4 * q : 4 * q + 4, :].bitcast(I32),
-            )
+        def load_x(z, tag):
+            table = keep.tile([P, T], I32, name=f"x_table{z}", tag=tag, align_bytes=64)
+            nc.sync.dma_start(out=table[:], in_=x_words[z].rearrange("p n r -> p (n r)").bitcast(I32))
+            return table
+
+        x_table = [load_x(0, "slot_w2_codes")]
 
         warm = keep.tile([P, 8], F32, name="warm")
         nc.vector.memset(warm[:, 0:4], 0.0)
         nc.scalar.activation(warm[:, 4:8], warm[:, 0:4], GELU)
 
-        x_planes = keep.tile([P, S], U8, name="x_planes", align_bytes=64)
-        nc.vector.tensor_copy(x_planes[:], xs_table[:].indirect(offsets[:]))
+        xs_picked = keep.tile([P, S], U8, name="xs_picked", align_bytes=64)
+        nc.vector.tensor_copy(xs_picked[:], xs_table[:].indirect(offsets[:]))
+        x_planes = keep.tile([P, PASSES, S], U8, name="x_planes", align_bytes=64)
+        nc.vector.memset(x_planes[:].rearrange("p z s -> p (z s)").bitcast(I32), 0)
+        for q in range(QUADS):
+            nc.scalar.dma_start(
+                out=x_planes[QUAD * q : QUAD * q + 4, :, :].bitcast(I32),
+                in_=xs_picked[8 * q : 8 * q + 8, :].bitcast(I32),
+            )
+        x_table.append(load_x(1, "slot_x1"))
 
         w1_codes, w1_plane = [], []
         for z in range(PASSES):
-            grouped = keep.tile([P, PACK * H], BF16, name=f"w1_grouped{z}", align_bytes=64)
-            copy = nc.scalar.copy if z == 0 else nc.vector.tensor_copy
-            copy(
+            grouped = keep.tile([P, PACK * H], BF16, name=f"w1_grouped{z}", tag=f"slot_pe{2 * z + 1}", align_bytes=64)
+            nc.scalar.copy(
                 out=grouped[:].rearrange("p (t m j) -> p m j t", t=PACK, j=PACK),
                 in_=w1_raw[z][:].rearrange("p j (m t) -> p m j t", t=PACK),
             )
@@ -91,11 +82,26 @@ def tile_picked_posadd_gelu_p_kernel(
             w1_codes.append(codes)
             w1_plane.append(plane)
 
+        pe_rows = pe.rearrange("(p t) c -> p t c", t=PACK)
+        pe_table = [keep.tile([P, T], F32, name=f"pe_table{t}", tag=f"slot_pe{t}", align_bytes=64) for t in range(PACK)]
+        for t in range(PACK):
+            nc.sync.dma_start(out=pe_table[t][:], in_=pe_rows[:, t, :])
+
         x_codes = []
         for z in range(PASSES):
             picked = keep.tile([P, S], U32, name=f"x_codes{z}", align_bytes=64)
             nc.vector.tensor_copy(picked[:], x_table[z][:].bitcast(U32).indirect(offsets[:]))
             x_codes.append(picked)
+
+        w2_codes = keep.tile([P, N], I32, name="w2_codes", tag="slot_w2_codes", align_bytes=64)
+        nc.sync.dma_start(out=w2_codes[:], in_=w2_words[0].rearrange("p n r -> p (n r)").bitcast(I32))
+        w2_plane = keep.tile([P, N], U8, name="w2_plane", tag="slot_x1", align_bytes=64)
+        nc.vector.memset(w2_plane[:].bitcast(I32), 0)
+        for q in range(QUADS):
+            nc.sync.dma_start(
+                out=w2_plane[QUAD * q : QUAD * q + 4, :].bitcast(I32),
+                in_=w2_scales[0, 4 * q : 4 * q + 4, :].bitcast(I32),
+            )
 
         acc = [psum.tile([P, S], F32, name=f"acc{t}", tag=f"acc{t}") for t in range(PACK)]
         for z in range(PASSES):
@@ -106,7 +112,7 @@ def tile_picked_posadd_gelu_p_kernel(
                     lhsT=w1_codes[z][:, cols].bitcast(FP8X4),
                     lhsT_scale=w1_plane[z][:, cols],
                     rhs=x_codes[z][:].bitcast(FP8X4),
-                    rhs_scale=x_planes[4 * z : P, :],
+                    rhs_scale=x_planes[:, z, :],
                     start=(z == 0),
                     stop=(z == PASSES - 1),
                 )
@@ -114,7 +120,9 @@ def tile_picked_posadd_gelu_p_kernel(
         for t in range(PACK):
             nc.scalar.copy(first[t][:], acc[t][:])
 
-        hidden = [keep.tile([P, PIECE, PACK], BF16, name=f"hidden{c}", align_bytes=64) for c in range(PIECES)]
+        starts = [sum(WIDTHS[:c]) for c in range(len(WIDTHS))]
+        pieces = list(enumerate(zip(starts, WIDTHS)))
+        hidden = [keep.tile([P, width, PACK], BF16, name=f"hidden{c}", align_bytes=64) for c, (j0, width) in pieces]
 
         def look_up(summed, t, j0, width):
             entries = offsets[:, j0 // LIST_ROWS : (j0 + width) // LIST_ROWS]
@@ -123,31 +131,31 @@ def tile_picked_posadd_gelu_p_kernel(
         early = keep.tile([P, 2, S], F32, name="early")
         for t in range(2):
             look_up(early[:, t, :], t, 0, S)
-        for c in range(PIECES):
-            cols = slice(c * PIECE, (c + 1) * PIECE)
-            nc.scalar.activation(hidden[c][:, :, 0:2], early[:, :, cols].rearrange("p t j -> p j t"), GELU)
-        late = [keep.tile([P, 2, PIECE], F32, name=f"late{c}") for c in range(PIECES)]
-        for c in range(PIECES):
-            look_up(late[c][:, 0, :], 2, c * PIECE, PIECE)
-        for c in range(PIECES):
-            look_up(late[c][:, 1, :], 3, c * PIECE, PIECE)
+        for c, (j0, width) in pieces:
+            nc.scalar.activation(
+                hidden[c][:, :, 0:2], early[:, :, j0 : j0 + width].rearrange("p t j -> p j t"), GELU
+            )
+        late = [keep.tile([P, 2, width], F32, name=f"late{c}") for c, (j0, width) in pieces]
+        for c, (j0, width) in pieces:
+            look_up(late[c][:, 0, :], 2, j0, width)
+        for c, (j0, width) in pieces:
+            look_up(late[c][:, 1, :], 3, j0, width)
             nc.scalar.activation(hidden[c][:, :, 2:4], late[c][:].rearrange("p t j -> p j t"), GELU)
 
         out_rows = out.rearrange("(u p) j -> p u j", p=P)
-        for c in range(PIECES):
-            cols = slice(c * PIECE, (c + 1) * PIECE)
-            h_codes = keep.tile([P, PIECE], U32, name=f"h_codes{c}", align_bytes=64)
-            h_plane = keep.tile([P, PIECE], U8, name=f"h_plane{c}", align_bytes=64)
+        for c, (j0, width) in pieces:
+            h_codes = keep.tile([P, width], U32, name=f"h_codes{c}", align_bytes=64)
+            h_plane = keep.tile([P, width], U8, name=f"h_plane{c}", align_bytes=64)
             nc.vector.quantize_mx(
                 out=h_codes[:].bitcast(FP8X4), scales=h_plane[:], in_=hidden[c][:].rearrange("p j t -> p (j t)")
             )
-            last = c == PIECES - 1
-            result = keep.tile([P, N // P, PIECE], F32, name=f"result{c}")
+            last = c == len(WIDTHS) - 1
+            result = keep.tile([P, N // P, width], F32, name=f"result{c}")
             if last:
-                banks = [psum.tile([P, PIECE], F32, name=f"product{c}"), psum.tile([P, PIECE], F32, name="tail", tag="acc0")]
+                banks = [psum.tile([P, width], F32, name=f"tail{u}", tag=f"acc{u}") for u in range(N // P)]
                 products = [bank[:] for bank in banks]
             else:
-                bank = psum.tile([P, N // P, PIECE], F32, name=f"product{c}")
+                bank = psum.tile([P, N // P, width], F32, name=f"product{c}")
                 products = [bank[:, u, :] for u in range(N // P)]
             for u in range(N // P):
                 rows = slice(u * P, (u + 1) * P)
@@ -163,6 +171,8 @@ def tile_picked_posadd_gelu_p_kernel(
             if last:
                 nc.vector.tensor_copy(result[:, 0, :], products[0])
                 nc.scalar.copy(result[:, 1, :], products[1])
+            elif c in ():
+                nc.vector.tensor_copy(result[:], bank[:])
             else:
                 nc.scalar.copy(result[:], bank[:])
-            nc.sync.dma_start(out=out_rows[:, :, cols], in_=result[:])
+            nc.sync.dma_start(out=out_rows[:, :, j0 : j0 + width], in_=result[:])

@@ -33,6 +33,13 @@ def tile_picked_posadd_gelu_p_kernel(
         keep = ctx.enter_context(tc.tile_pool(name="keep", bufs=1))
         psum = ctx.enter_context(tc.psum_pool(name="psum", bufs=1))
 
+        w1_raw = [keep.tile([P, PACK, H], F32, name=f"w1_raw{z}", tag=f"slot_pe{2 * z}", align_bytes=64) for z in range(PASSES)]
+
+        def load_w1(z):
+            rows = w1[z * K_PASS : (z + 1) * K_PASS, :]
+            nc.sync.dma_start(out=w1_raw[z][:], in_=rows.rearrange("(p j) c -> p j c", j=PACK))
+
+        load_w1(0)
         offsets = keep.tile([P, S // LIST_ROWS], U16, name="offsets")
         nc.sync.dma_start(offsets[:], offs)
 
@@ -42,10 +49,7 @@ def tile_picked_posadd_gelu_p_kernel(
         for z in range(PASSES):
             nc.sync.dma_start(out=xs_table[z:QUAD:PASSES, :].bitcast(I32), in_=x_scales[z].bitcast(I32))
 
-        w1_raw = [keep.tile([P, PACK, H], F32, name=f"w1_raw{z}", tag=f"slot_pe{2 * z}", align_bytes=64) for z in range(PASSES)]
-        for z in range(PASSES):
-            rows = w1[z * K_PASS : (z + 1) * K_PASS, :]
-            nc.sync.dma_start(out=w1_raw[z][:], in_=rows.rearrange("(p j) c -> p j c", j=PACK))
+        load_w1(1)
 
         def load_x(z, tag):
             table = keep.tile([P, T], I32, name=f"x_table{z}", tag=tag, align_bytes=64)

@@ -47,7 +47,7 @@ def tile_picked_posadd_gelu_p_kernel(
         nc.vector.memset(xs_table[QUAD : 2 * QUAD, :].bitcast(I32), 0)
         nc.vector.memset(xs_table[2 * QUAD : P, :].bitcast(I32), 0)
         for z in range(PASSES):
-            nc.sync.dma_start(out=xs_table[z:QUAD:PASSES, :].bitcast(I32), in_=x_scales[z].bitcast(I32))
+            nc.scalar.dma_start(out=xs_table[z:QUAD:PASSES, :].bitcast(I32), in_=x_scales[z].bitcast(I32))
 
         load_w1(1)
 

@@ -146,25 +146,20 @@ def tile_picked_posadd_gelu_p_kernel(
             look_up(late[c][:, 1, :], 3, j0, width)
             nc.scalar.activation(hidden[c][:, :, 2:4], late[c][:].rearrange("p t j -> p j t"), GELU)
 
-        out_rows = out.rearrange("(u p) j -> p u j", p=P)
         for c, (j0, width) in pieces:
             h_codes = keep.tile([P, width], U32, name=f"h_codes{c}", align_bytes=64)
             h_plane = keep.tile([P, width], U8, name=f"h_plane{c}", align_bytes=64)
             nc.vector.quantize_mx(
                 out=h_codes[:].bitcast(FP8X4), scales=h_plane[:], in_=hidden[c][:].rearrange("p j t -> p (j t)")
             )
-            last = c == len(WIDTHS) - 1
-            result = keep.tile([P, N // P, width], F32, name=f"result{c}")
-            if last:
-                banks = [psum.tile([P, width], F32, name=f"tail{u}", tag=f"acc{u}") for u in range(N // P)]
-                products = [bank[:] for bank in banks]
-            else:
-                bank = psum.tile([P, N // P, width], F32, name=f"product{c}")
-                products = [bank[:, u, :] for u in range(N // P)]
+            if c % 2 == 0:
+                result = [keep.tile([P, 2 * width], F32, name=f"result{c}_{u}") for u in range(N // P)]
+            cols = slice((c % 2) * width, (c % 2 + 1) * width)
             for u in range(N // P):
                 rows = slice(u * P, (u + 1) * P)
+                bank = psum.tile([P, width], F32, name=f"product{c}_{u}", tag=f"acc{(2 * c + u + PACK) % (2 * PACK)}")
                 nc.tensor.matmul_mx(
-                    out=products[u],
+                    out=bank[:],
                     lhsT=w2_codes[:, rows].bitcast(FP8X4),
                     lhsT_scale=w2_plane[:, rows],
                     rhs=h_codes[:].bitcast(FP8X4),
@@ -172,11 +167,6 @@ def tile_picked_posadd_gelu_p_kernel(
                     start=True,
                     stop=True,
                 )
-            if last:
-                nc.vector.tensor_copy(result[:, 0, :], products[0])
-                nc.scalar.copy(result[:, 1, :], products[1])
-            elif c in ():
-                nc.vector.tensor_copy(result[:], bank[:])
-            else:
-                nc.scalar.copy(result[:], bank[:])
-            nc.sync.dma_start(out=out_rows[:, :, j0 : j0 + width], in_=result[:])
+                (nc.scalar.copy, nc.vector.tensor_copy)[u](result[u][:, cols], bank[:])
+                if c % 2 == 1:
+                    nc.sync.dma_start(out=out[rows, j0 - width : j0 + width], in_=result[u][:])

@@ -143,8 +143,12 @@ def tile_picked_posadd_gelu_p_kernel(
         for c, (j0, width) in pieces:
             look_up(late[c][:, 0, :], 2, j0, width)
         for c, (j0, width) in pieces:
-            look_up(late[c][:, 1, :], 3, j0, width)
-            nc.scalar.activation(hidden[c][:, :, 2:4], late[c][:].rearrange("p t j -> p j t"), GELU)
+            step = width // 2 if c == 0 else width
+            for a in range(0, width, step):
+                look_up(late[c][:, 1, a : a + step], 3, j0 + a, step)
+                nc.scalar.activation(
+                    hidden[c][:, a : a + step, 2:4], late[c][:, :, a : a + step].rearrange("p t j -> p j t"), GELU
+                )
 
         for c, (j0, width) in pieces:
             h_codes = keep.tile([P, width], U32, name=f"h_codes{c}", align_bytes=64)

@@ -33,30 +33,17 @@ def tile_picked_posadd_gelu_p_kernel(
         keep = ctx.enter_context(tc.tile_pool(name="keep", bufs=1))
         psum = ctx.enter_context(tc.psum_pool(name="psum", bufs=1))
 
-        w1_raw = [keep.tile([P, PACK, H], F32, name=f"w1_raw{z}", tag=f"slot_pe{2 * z}", align_bytes=64) for z in range(PASSES)]
-
-        def load_w1(z):
-            rows = w1[z * K_PASS : (z + 1) * K_PASS, :]
-            nc.sync.dma_start(out=w1_raw[z][:], in_=rows.rearrange("(p j) c -> p j c", j=PACK))
-
-        load_w1(0)
-        offsets = keep.tile([P, S // LIST_ROWS], U16, name="offsets")
-        nc.sync.dma_start(offsets[:], offs)
-
-        xs_table = keep.tile([P, T], U8, name="xs_table", tag="slot_x1", align_bytes=64)
+        xs_table = keep.tile([P, T], U8, name="xs_table", align_bytes=64)
         nc.vector.memset(xs_table[QUAD : 2 * QUAD, :].bitcast(I32), 0)
         nc.vector.memset(xs_table[2 * QUAD : P, :].bitcast(I32), 0)
-        for z in range(PASSES):
-            nc.scalar.dma_start(out=xs_table[z:QUAD:PASSES, :].bitcast(I32), in_=x_scales[z].bitcast(I32))
+        nc.sync.dma_start(out=xs_table[0:QUAD, :].bitcast(I32), in_=x_scales.bitcast(I32).rearrange("z b t -> b z t"))
+        offsets = keep.tile([P, S // LIST_ROWS], U16, name="offsets")
+        nc.sync.dma_start(offsets[:], offs)
+        w1_raw = keep.tile([P, PASSES, PACK * H], F32, name="w1_raw", tag="slot_pe1", align_bytes=64)
+        nc.sync.dma_start(out=w1_raw[:], in_=w1.rearrange("(z p j) c -> p z (j c)", z=PASSES, j=PACK))
 
-        load_w1(1)
-
-        def load_x(z, tag):
-            table = keep.tile([P, T], I32, name=f"x_table{z}", tag=tag, align_bytes=64)
-            nc.sync.dma_start(out=table[:], in_=x_words[z].rearrange("p n r -> p (n r)").bitcast(I32))
-            return table
-
-        x_table = [load_x(0, "slot_w2_codes")]
+        x_table = keep.tile([P, PASSES, T], I32, name="x_table", tag="slot_pe3", align_bytes=64)
+        nc.sync.dma_start(out=x_table[:], in_=x_words.rearrange("z p n r -> p z (n r)").bitcast(I32))
 
         warm = keep.tile([P, 8], F32, name="warm")
         nc.vector.memset(warm[:, 0:4], 0.0)
@@ -71,45 +58,34 @@ def tile_picked_posadd_gelu_p_kernel(
                 out=x_planes[QUAD * q : QUAD * q + 4, :, :].bitcast(I32),
                 in_=xs_picked[8 * q : 8 * q + 8, :].bitcast(I32),
             )
-        x_table.append(load_x(1, "slot_x1"))
 
         w1_codes, w1_plane = [], []
         for z in range(PASSES):
-            grouped = keep.tile([P, PACK * H], BF16, name=f"w1_grouped{z}", tag=f"slot_pe{2 * z + 1}", align_bytes=64)
-            nc.scalar.copy(
-                out=grouped[:].rearrange("p (t m j) -> p m j t", t=PACK, j=PACK),
-                in_=w1_raw[z][:].rearrange("p j (m t) -> p m j t", t=PACK),
+            grouped = keep.tile([P, PACK * H], BF16, name=f"w1_grouped{z}", tag=f"slot_pe{2 * z}", align_bytes=64)
+            (nc.vector.tensor_copy, nc.scalar.copy)[z](
+                grouped[:].rearrange("p (t m j) -> p m t j", t=PACK, j=PACK),
+                w1_raw[:, z, :].rearrange("p (j m t) -> p m t j", j=PACK, t=PACK),
             )
-            codes = keep.tile([P, H], U32, name=f"w1_codes{z}", align_bytes=64)
+            codes = keep.tile([P, H], U32, name=f"w1_codes{z}", tag=f"slot_w2_{z}", align_bytes=64)
             plane = keep.tile([P, H], U8, name=f"w1_plane{z}", align_bytes=64)
             nc.vector.quantize_mx(out=codes[:].bitcast(FP8X4), scales=plane[:], in_=grouped[:])
             w1_codes.append(codes)
             w1_plane.append(plane)
+
+        x_codes = []
+        for z in range(PASSES):
+            picked = keep.tile([P, S], U32, name=f"x_codes{z}", align_bytes=64)
+            nc.vector.tensor_copy(picked[:], x_table[:, z, :].bitcast(U32).indirect(offsets[:]))
+            x_codes.append(picked)
 
         pe_rows = pe.rearrange("(p t) c -> p t c", t=PACK)
         pe_table = [keep.tile([P, T], F32, name=f"pe_table{t}", tag=f"slot_pe{t}", align_bytes=64) for t in range(PACK)]
         for t in range(PACK):
             nc.sync.dma_start(out=pe_table[t][:], in_=pe_rows[:, t, :])
 
-        x_codes = []
-        for z in range(PASSES):
-            picked = keep.tile([P, S], U32, name=f"x_codes{z}", align_bytes=64)
-            nc.vector.tensor_copy(picked[:], x_table[z][:].bitcast(U32).indirect(offsets[:]))
-            x_codes.append(picked)
-
-        w2_codes = keep.tile([P, N], I32, name="w2_codes", tag="slot_w2_codes", align_bytes=64)
-        nc.sync.dma_start(out=w2_codes[:], in_=w2_words[0].rearrange("p n r -> p (n r)").bitcast(I32))
-        w2_plane = keep.tile([P, N], U8, name="w2_plane", tag="slot_x1", align_bytes=64)
-        nc.vector.memset(w2_plane[:].bitcast(I32), 0)
-        for q in range(QUADS):
-            nc.sync.dma_start(
-                out=w2_plane[QUAD * q : QUAD * q + 4, :].bitcast(I32),
-                in_=w2_scales[0, 4 * q : 4 * q + 4, :].bitcast(I32),
-            )
-
         acc = [psum.tile([P, S], F32, name=f"acc{t}", tag=f"acc{t}") for t in range(PACK)]
-        for z in range(PASSES):
-            for t in range(PACK):
+        for t in range(PACK):
+            for z in range(PASSES):
                 cols = slice(t * P, (t + 1) * P)
                 nc.tensor.matmul_mx(
                     out=acc[t][:],
@@ -120,9 +96,19 @@ def tile_picked_posadd_gelu_p_kernel(
                     start=(z == 0),
                     stop=(z == PASSES - 1),
                 )
-        first = [keep.tile([P, S], F32, name=f"first{t}") for t in range(PACK)]
-        for t in range(PACK):
+        first = {t: keep.tile([P, S], F32, name=f"first{t}") for t in range(1, PACK)}
+        for t in range(1, PACK):
             nc.scalar.copy(first[t][:], acc[t][:])
+
+        w2_codes = keep.tile([P, N], I32, name="w2_codes", tag="slot_w2_0", align_bytes=64)
+        nc.sync.dma_start(out=w2_codes[:], in_=w2_words[0].rearrange("p n r -> p (n r)").bitcast(I32))
+        w2_plane = keep.tile([P, N], U8, name="w2_plane", tag="slot_w2_1", align_bytes=64)
+        nc.vector.memset(w2_plane[:].bitcast(I32), 0)
+        for q in range(QUADS):
+            nc.sync.dma_start(
+                out=w2_plane[QUAD * q : QUAD * q + 4, :].bitcast(I32),
+                in_=w2_scales[0, 4 * q : 4 * q + 4, :].bitcast(I32),
+            )
 
         starts = [sum(WIDTHS[:c]) for c in range(len(WIDTHS))]
         pieces = list(enumerate(zip(starts, WIDTHS)))
@@ -133,8 +119,10 @@ def tile_picked_posadd_gelu_p_kernel(
             nc.vector.tensor_tensor(summed, pe_table[t][:].indirect(entries), first[t][:, j0 : j0 + width], ADD)
 
         early = keep.tile([P, 2, S], F32, name="early")
-        for t in range(2):
-            look_up(early[:, t, :], t, 0, S)
+        pe_picked = keep.tile([P, S], F32, name="pe_picked")
+        nc.vector.tensor_copy(pe_picked[:], pe_table[0][:].indirect(offsets[:]))
+        nc.vector.tensor_tensor(early[:, 0, :], acc[0][:], pe_picked[:], ADD)
+        look_up(early[:, 1, :], 1, 0, S)
         for c, (j0, width) in pieces:
             nc.scalar.activation(
                 hidden[c][:, :, 0:2], early[:, :, j0 : j0 + width].rearrange("p t j -> p j t"), GELU

@@ -33,17 +33,20 @@ def tile_picked_posadd_gelu_p_kernel(
         keep = ctx.enter_context(tc.tile_pool(name="keep", bufs=1))
         psum = ctx.enter_context(tc.psum_pool(name="psum", bufs=1))
 
-        xs_table = keep.tile([P, T], U8, name="xs_table", align_bytes=64)
+        xs_table = keep.tile([P, T], U8, name="xs_table", tag="slot_pe0", align_bytes=64)
         nc.vector.memset(xs_table[QUAD : 2 * QUAD, :].bitcast(I32), 0)
         nc.vector.memset(xs_table[2 * QUAD : P, :].bitcast(I32), 0)
         nc.sync.dma_start(out=xs_table[0:QUAD, :].bitcast(I32), in_=x_scales.bitcast(I32).rearrange("z b t -> b z t"))
         offsets = keep.tile([P, S // LIST_ROWS], U16, name="offsets")
         nc.sync.dma_start(offsets[:], offs)
-        w1_raw = keep.tile([P, PASSES, PACK * H], F32, name="w1_raw", tag="slot_pe1", align_bytes=64)
+        w1_raw = keep.tile([P, PASSES, PACK * H], F32, name="w1_raw", tag="slot_pe2", align_bytes=64)
         nc.sync.dma_start(out=w1_raw[:], in_=w1.rearrange("(z p j) c -> p z (j c)", z=PASSES, j=PACK))
 
-        x_table = keep.tile([P, PASSES, T], I32, name="x_table", tag="slot_pe3", align_bytes=64)
-        nc.sync.dma_start(out=x_table[:], in_=x_words.rearrange("z p n r -> p z (n r)").bitcast(I32))
+        x_table = []
+        for z in range(PASSES):
+            table = keep.tile([P, T], I32, name=f"x_table{z}", tag=f"slot_w2_{z}", align_bytes=64)
+            nc.sync.dma_start(out=table[:], in_=x_words[z].rearrange("p n r -> p (n r)").bitcast(I32))
+            x_table.append(table)
 
         warm = keep.tile([P, 8], F32, name="warm")
         nc.vector.memset(warm[:, 0:4], 0.0)
@@ -54,19 +57,19 @@ def tile_picked_posadd_gelu_p_kernel(
         x_planes = keep.tile([P, PASSES, S], U8, name="x_planes", align_bytes=64)
         nc.vector.memset(x_planes[:].rearrange("p z s -> p (z s)").bitcast(I32), 0)
         for q in range(QUADS):
-            nc.scalar.dma_start(
+            nc.sync.dma_start(
                 out=x_planes[QUAD * q : QUAD * q + 4, :, :].bitcast(I32),
                 in_=xs_picked[8 * q : 8 * q + 8, :].bitcast(I32),
             )
 
         w1_codes, w1_plane = [], []
         for z in range(PASSES):
-            grouped = keep.tile([P, PACK * H], BF16, name=f"w1_grouped{z}", tag=f"slot_pe{2 * z}", align_bytes=64)
+            grouped = keep.tile([P, PACK * H], BF16, name=f"w1_grouped{z}", tag=f"slot_pe{2 * z + 1}", align_bytes=64)
             (nc.vector.tensor_copy, nc.scalar.copy)[z](
                 grouped[:].rearrange("p (t m j) -> p m t j", t=PACK, j=PACK),
                 w1_raw[:, z, :].rearrange("p (j m t) -> p m t j", j=PACK, t=PACK),
             )
-            codes = keep.tile([P, H], U32, name=f"w1_codes{z}", tag=f"slot_w2_{z}", align_bytes=64)
+            codes = keep.tile([P, H], U32, name=f"w1_codes{z}", align_bytes=64)
             plane = keep.tile([P, H], U8, name=f"w1_plane{z}", align_bytes=64)
             nc.vector.quantize_mx(out=codes[:].bitcast(FP8X4), scales=plane[:], in_=grouped[:])
             w1_codes.append(codes)
@@ -75,7 +78,7 @@ def tile_picked_posadd_gelu_p_kernel(
         x_codes = []
         for z in range(PASSES):
             picked = keep.tile([P, S], U32, name=f"x_codes{z}", align_bytes=64)
-            nc.vector.tensor_copy(picked[:], x_table[:, z, :].bitcast(U32).indirect(offsets[:]))
+            nc.vector.tensor_copy(picked[:], x_table[z][:].bitcast(U32).indirect(offsets[:]))
             x_codes.append(picked)
 
         pe_rows = pe.rearrange("(p t) c -> p t c", t=PACK)
@@ -96,8 +99,8 @@ def tile_picked_posadd_gelu_p_kernel(
                     start=(z == 0),
                     stop=(z == PASSES - 1),
                 )
-        first = {t: keep.tile([P, S], F32, name=f"first{t}") for t in range(1, PACK)}
-        for t in range(1, PACK):
+        first = [keep.tile([P, S], F32, name=f"first{t}") for t in range(PACK)]
+        for t in range(PACK):
             nc.scalar.copy(first[t][:], acc[t][:])
 
         w2_codes = keep.tile([P, N], I32, name="w2_codes", tag="slot_w2_0", align_bytes=64)
@@ -119,10 +122,8 @@ def tile_picked_posadd_gelu_p_kernel(
             nc.vector.tensor_tensor(summed, pe_table[t][:].indirect(entries), first[t][:, j0 : j0 + width], ADD)
 
         early = keep.tile([P, 2, S], F32, name="early")
-        pe_picked = keep.tile([P, S], F32, name="pe_picked")
-        nc.vector.tensor_copy(pe_picked[:], pe_table[0][:].indirect(offsets[:]))
-        nc.vector.tensor_tensor(early[:, 0, :], acc[0][:], pe_picked[:], ADD)
-        look_up(early[:, 1, :], 1, 0, S)
+        for t in range(2):
+            look_up(early[:, t, :], t, 0, S)
         for c, (j0, width) in pieces:
             nc.scalar.activation(
                 hidden[c][:, :, 0:2], early[:, :, j0 : j0 + width].rearrange("p t j -> p j t"), GELU

@@ -1,3 +1,4 @@
+import itertools
 from contextlib import ExitStack
 
 import concourse.mybir as mybir
@@ -33,20 +34,23 @@ def tile_picked_posadd_gelu_p_kernel(
         keep = ctx.enter_context(tc.tile_pool(name="keep", bufs=1))
         psum = ctx.enter_context(tc.psum_pool(name="psum", bufs=1))
 
+        def load_x(z, tag):
+            table = keep.tile([P, T], I32, name=f"x_table{z}", tag=tag, align_bytes=64)
+            nc.sync.dma_start(out=table[:], in_=x_words[z].rearrange("p n r -> p (n r)").bitcast(I32))
+            return table
+
+        x_table = [load_x(0, "x_table0")]
+        offsets = keep.tile([P, S // LIST_ROWS], U16, name="offsets")
+        nc.sync.dma_start(offsets[:], offs)
+
         xs_table = keep.tile([P, T], U8, name="xs_table", tag="slot_pe0", align_bytes=64)
         nc.vector.memset(xs_table[QUAD : 2 * QUAD, :].bitcast(I32), 0)
         nc.vector.memset(xs_table[2 * QUAD : P, :].bitcast(I32), 0)
-        nc.sync.dma_start(out=xs_table[0:QUAD, :].bitcast(I32), in_=x_scales.bitcast(I32).rearrange("z b t -> b z t"))
-        offsets = keep.tile([P, S // LIST_ROWS], U16, name="offsets")
-        nc.sync.dma_start(offsets[:], offs)
+        nc.scalar.dma_start(out=xs_table[0:QUAD, :].bitcast(I32), in_=x_scales.bitcast(I32).rearrange("z b t -> b z t"))
+
         w1_raw = keep.tile([P, PASSES, PACK * H], F32, name="w1_raw", tag="slot_pe2", align_bytes=64)
         nc.sync.dma_start(out=w1_raw[:], in_=w1.rearrange("(z p j) c -> p z (j c)", z=PASSES, j=PACK))
-
-        x_table = []
-        for z in range(PASSES):
-            table = keep.tile([P, T], I32, name=f"x_table{z}", tag=f"slot_w2_{z}", align_bytes=64)
-            nc.sync.dma_start(out=table[:], in_=x_words[z].rearrange("p n r -> p (n r)").bitcast(I32))
-            x_table.append(table)
+        x_table.append(load_x(1, "slot_w2_1"))
 
         warm = keep.tile([P, 8], F32, name="warm")
         nc.vector.memset(warm[:, 0:4], 0.0)
@@ -64,12 +68,12 @@ def tile_picked_posadd_gelu_p_kernel(
 
         w1_codes, w1_plane = [], []
         for z in range(PASSES):
-            grouped = keep.tile([P, PACK * H], BF16, name=f"w1_grouped{z}", tag=f"slot_pe{2 * z + 1}", align_bytes=64)
+            grouped = keep.tile([P, PACK * H], BF16, name=f"w1_grouped{z}", tag=("slot_pe1", "slot_pe3")[z], align_bytes=64)
             (nc.vector.tensor_copy, nc.scalar.copy)[z](
                 grouped[:].rearrange("p (t m j) -> p m t j", t=PACK, j=PACK),
                 w1_raw[:, z, :].rearrange("p (j m t) -> p m t j", j=PACK, t=PACK),
             )
-            codes = keep.tile([P, H], U32, name=f"w1_codes{z}", align_bytes=64)
+            codes = keep.tile([P, H], U32, name=f"w1_codes{z}", tag=("w1_codes0", "slot_w2_0")[z], align_bytes=64)
             plane = keep.tile([P, H], U8, name=f"w1_plane{z}", align_bytes=64)
             nc.vector.quantize_mx(out=codes[:].bitcast(FP8X4), scales=plane[:], in_=grouped[:])
             w1_codes.append(codes)
@@ -87,8 +91,8 @@ def tile_picked_posadd_gelu_p_kernel(
             nc.sync.dma_start(out=pe_table[t][:], in_=pe_rows[:, t, :])
 
         acc = [psum.tile([P, S], F32, name=f"acc{t}", tag=f"acc{t}") for t in range(PACK)]
-        for t in range(PACK):
-            for z in range(PASSES):
+        for pair in range(0, PACK, 2):
+            for z, t in itertools.product(range(PASSES), (pair, pair + 1)):
                 cols = slice(t * P, (t + 1) * P)
                 nc.tensor.matmul_mx(
                     out=acc[t][:],

@@ -44,9 +44,9 @@ def tile_picked_posadd_gelu_p_kernel(
         nc.sync.dma_start(offsets[:], offs)
 
         xs_table = keep.tile([P, T], U8, name="xs_table", tag="slot_pe0", align_bytes=64)
-        nc.vector.memset(xs_table[QUAD : 2 * QUAD, :].bitcast(I32), 0)
-        nc.vector.memset(xs_table[2 * QUAD : P, :].bitcast(I32), 0)
-        nc.scalar.dma_start(out=xs_table[0:QUAD, :].bitcast(I32), in_=x_scales.bitcast(I32).rearrange("z b t -> b z t"))
+        nc.vector.memset(xs_table[0 : 2 * QUAD, :].bitcast(I32), 0)
+        nc.vector.memset(xs_table[3 * QUAD : P, :].bitcast(I32), 0)
+        nc.scalar.dma_start(out=xs_table[2 * QUAD : 3 * QUAD, :].bitcast(I32), in_=x_scales.bitcast(I32).rearrange("z b t -> b z t"))
 
         w1_raw = keep.tile([P, PASSES, PACK * H], F32, name="w1_raw", tag="slot_pe2", align_bytes=64)
         nc.sync.dma_start(out=w1_raw[:], in_=w1.rearrange("(z p j) c -> p z (j c)", z=PASSES, j=PACK))
@@ -63,7 +63,7 @@ def tile_picked_posadd_gelu_p_kernel(
         for q in range(QUADS):
             nc.sync.dma_start(
                 out=x_planes[QUAD * q : QUAD * q + 4, :, :].bitcast(I32),
-                in_=xs_picked[8 * q : 8 * q + 8, :].bitcast(I32),
+                in_=xs_picked[2 * QUAD + 8 * q : 2 * QUAD + 8 * q + 8, :].bitcast(I32),
             )
 
         w1_codes, w1_plane = [], []

@@ -52,10 +52,6 @@ def tile_picked_posadd_gelu_p_kernel(
         nc.sync.dma_start(out=w1_raw[:], in_=w1.rearrange("(z p j) c -> p z (j c)", z=PASSES, j=PACK))
         x_table.append(load_x(1, "slot_w2_1"))
 
-        warm = keep.tile([P, 8], F32, name="warm")
-        nc.vector.memset(warm[:, 0:4], 0.0)
-        nc.scalar.activation(warm[:, 4:8], warm[:, 0:4], GELU)
-
         xs_picked = keep.tile([P, S], U8, name="xs_picked", align_bytes=64)
         nc.vector.tensor_copy(xs_picked[:], xs_table[:].indirect(offsets[:]))
         x_planes = keep.tile([P, PASSES, S], U8, name="x_planes", align_bytes=64)

@@ -56,7 +56,7 @@ def tile_picked_posadd_gelu_p_kernel(
         nc.vector.tensor_copy(xs_picked[:], xs_table[:].indirect(offsets[:]))
         x_planes = keep.tile([P, PASSES, S], U8, name="x_planes", align_bytes=64)
         nc.vector.memset(x_planes[:].rearrange("p z s -> p (z s)").bitcast(I32), 0)
-        for q in range(QUADS):
+        for q in (0, 2, 1, 3):
             nc.sync.dma_start(
                 out=x_planes[QUAD * q : QUAD * q + 4, :, :].bitcast(I32),
                 in_=xs_picked[2 * QUAD + 8 * q : 2 * QUAD + 8 * q + 8, :].bitcast(I32),
@@ -107,7 +107,7 @@ def tile_picked_posadd_gelu_p_kernel(
         nc.sync.dma_start(out=w2_codes[:], in_=w2_words[0].rearrange("p n r -> p (n r)").bitcast(I32))
         w2_plane = keep.tile([P, N], U8, name="w2_plane", tag="slot_w2_1", align_bytes=64)
         nc.vector.memset(w2_plane[:].bitcast(I32), 0)
-        for q in range(QUADS):
+        for q in (0, 2, 1, 3):
             nc.sync.dma_start(
                 out=w2_plane[QUAD * q : QUAD * q + 4, :].bitcast(I32),
                 in_=w2_scales[0, 4 * q : 4 * q + 4, :].bitcast(I32),

@@ -23,6 +23,7 @@ PASSES = K // K_PASS
 QUADS = 4
 QUAD = P // QUADS
 LIST_ROWS = 16
+ALIGN = 256
 WIDTHS = [128,128,128,128]
 
 
@@ -35,7 +36,7 @@ def tile_picked_posadd_gelu_p_kernel(
         psum = ctx.enter_context(tc.psum_pool(name="psum", bufs=1))
 
         def load_x(z, tag):
-            table = keep.tile([P, T], I32, name=f"x_table{z}", tag=tag, align_bytes=64)
+            table = keep.tile([P, T], I32, name=f"x_table{z}", tag=tag, align_bytes=ALIGN)
             nc.sync.dma_start(out=table[:], in_=x_words[z].rearrange("p n r -> p (n r)").bitcast(I32))
             return table
 
@@ -43,18 +44,18 @@ def tile_picked_posadd_gelu_p_kernel(
         offsets = keep.tile([P, S // LIST_ROWS], U16, name="offsets")
         nc.sync.dma_start(offsets[:], offs)
 
-        xs_table = keep.tile([P, T], U8, name="xs_table", tag="slot_pe0", align_bytes=64)
+        xs_table = keep.tile([P, T], U8, name="xs_table", tag="slot_pe0", align_bytes=ALIGN)
         nc.vector.memset(xs_table[0 : 2 * QUAD, :].bitcast(I32), 0)
         nc.vector.memset(xs_table[3 * QUAD : P, :].bitcast(I32), 0)
         nc.scalar.dma_start(out=xs_table[2 * QUAD : 3 * QUAD, :].bitcast(I32), in_=x_scales.bitcast(I32).rearrange("z b t -> b z t"))
 
-        w1_raw = keep.tile([P, PASSES, PACK * H], F32, name="w1_raw", tag="slot_pe2", align_bytes=64)
+        w1_raw = keep.tile([P, PASSES, PACK * H], F32, name="w1_raw", tag="slot_pe2", align_bytes=ALIGN)
         nc.sync.dma_start(out=w1_raw[:], in_=w1.rearrange("(z p j) c -> p z (j c)", z=PASSES, j=PACK))
         x_table.append(load_x(1, "slot_w2_1"))
 
-        xs_picked = keep.tile([P, S], U8, name="xs_picked", align_bytes=64)
+        xs_picked = keep.tile([P, S], U8, name="xs_picked", align_bytes=ALIGN)
         nc.vector.tensor_copy(xs_picked[:], xs_table[:].indirect(offsets[:]))
-        x_planes = keep.tile([P, PASSES, S], U8, name="x_planes", align_bytes=64)
+        x_planes = keep.tile([P, PASSES, S], U8, name="x_planes", align_bytes=ALIGN)
         nc.vector.memset(x_planes[:].rearrange("p z s -> p (z s)").bitcast(I32), 0)
         for q in (0, 2, 1, 3):
             nc.sync.dma_start(
@@ -64,25 +65,25 @@ def tile_picked_posadd_gelu_p_kernel(
 
         w1_codes, w1_plane = [], []
         for z in range(PASSES):
-            grouped = keep.tile([P, PACK * H], BF16, name=f"w1_grouped{z}", tag=("slot_pe1", "slot_pe3")[z], align_bytes=64)
+            grouped = keep.tile([P, PACK * H], BF16, name=f"w1_grouped{z}", tag=("slot_pe1", "slot_pe3")[z], align_bytes=ALIGN)
             (nc.vector.tensor_copy, nc.scalar.copy)[z](
                 grouped[:].rearrange("p (t m j) -> p m t j", t=PACK, j=PACK),
                 w1_raw[:, z, :].rearrange("p (j m t) -> p m t j", j=PACK, t=PACK),
             )
-            codes = keep.tile([P, H], U32, name=f"w1_codes{z}", tag=("w1_codes0", "slot_w2_0")[z], align_bytes=64)
-            plane = keep.tile([P, H], U8, name=f"w1_plane{z}", align_bytes=64)
+            codes = keep.tile([P, H], U32, name=f"w1_codes{z}", tag=("w1_codes0", "slot_w2_0")[z], align_bytes=ALIGN)
+            plane = keep.tile([P, H], U8, name=f"w1_plane{z}", align_bytes=ALIGN)
             nc.vector.quantize_mx(out=codes[:].bitcast(FP8X4), scales=plane[:], in_=grouped[:])
             w1_codes.append(codes)
             w1_plane.append(plane)
 
         x_codes = []
         for z in range(PASSES):
-            picked = keep.tile([P, S], U32, name=f"x_codes{z}", align_bytes=64)
+            picked = keep.tile([P, S], U32, name=f"x_codes{z}", align_bytes=ALIGN)
             nc.vector.tensor_copy(picked[:], x_table[z][:].bitcast(U32).indirect(offsets[:]))
             x_codes.append(picked)
 
         pe_rows = pe.rearrange("(p t) c -> p t c", t=PACK)
-        pe_table = [keep.tile([P, T], F32, name=f"pe_table{t}", tag=f"slot_pe{t}", align_bytes=64) for t in range(PACK)]
+        pe_table = [keep.tile([P, T], F32, name=f"pe_table{t}", tag=f"slot_pe{t}", align_bytes=ALIGN) for t in range(PACK)]
         for t in range(PACK):
             nc.sync.dma_start(out=pe_table[t][:], in_=pe_rows[:, t, :])
 
@@ -103,9 +104,9 @@ def tile_picked_posadd_gelu_p_kernel(
         for t in range(PACK):
             nc.scalar.copy(first[t][:], acc[t][:])
 
-        w2_codes = keep.tile([P, N], I32, name="w2_codes", tag="slot_w2_0", align_bytes=64)
+        w2_codes = keep.tile([P, N], I32, name="w2_codes", tag="slot_w2_0", align_bytes=ALIGN)
         nc.sync.dma_start(out=w2_codes[:], in_=w2_words[0].rearrange("p n r -> p (n r)").bitcast(I32))
-        w2_plane = keep.tile([P, N], U8, name="w2_plane", tag="slot_w2_1", align_bytes=64)
+        w2_plane = keep.tile([P, N], U8, name="w2_plane", tag="slot_w2_1", align_bytes=ALIGN)
         nc.vector.memset(w2_plane[:].bitcast(I32), 0)
         for q in (0, 2, 1, 3):
             nc.sync.dma_start(
@@ -115,7 +116,7 @@ def tile_picked_posadd_gelu_p_kernel(
 
         starts = [sum(WIDTHS[:c]) for c in range(len(WIDTHS))]
         pieces = list(enumerate(zip(starts, WIDTHS)))
-        hidden = [keep.tile([P, width, PACK], BF16, name=f"hidden{c}", align_bytes=64) for c, (j0, width) in pieces]
+        hidden = [keep.tile([P, width, PACK], BF16, name=f"hidden{c}", align_bytes=ALIGN) for c, (j0, width) in pieces]
 
         def look_up(summed, t, j0, width):
             entries = offsets[:, j0 // LIST_ROWS : (j0 + width) // LIST_ROWS]
@@ -140,13 +141,13 @@ def tile_picked_posadd_gelu_p_kernel(
                 )
 
         for c, (j0, width) in pieces:
-            h_codes = keep.tile([P, width], U32, name=f"h_codes{c}", align_bytes=64)
-            h_plane = keep.tile([P, width], U8, name=f"h_plane{c}", align_bytes=64)
+            h_codes = keep.tile([P, width], U32, name=f"h_codes{c}", align_bytes=ALIGN)
+            h_plane = keep.tile([P, width], U8, name=f"h_plane{c}", align_bytes=ALIGN)
             nc.vector.quantize_mx(
                 out=h_codes[:].bitcast(FP8X4), scales=h_plane[:], in_=hidden[c][:].rearrange("p j t -> p (j t)")
             )
             if c % 2 == 0:
-                result = [keep.tile([P, 2 * width], F32, name=f"result{c}_{u}") for u in range(N // P)]
+                result = [keep.tile([P, 2 * width], F32, name=f"result{c}_{u}", align_bytes=ALIGN) for u in range(N // P)]
             cols = slice((c % 2) * width, (c % 2 + 1) * width)
             for u in range(N // P):
                 rows = slice(u * P, (u + 1) * P)

@@ -129,7 +129,7 @@ def tile_picked_posadd_gelu_p_kernel(
             nc.scalar.activation(
                 hidden[c][:, :, 0:2], early[:, :, j0 : j0 + width].rearrange("p t j -> p j t"), GELU
             )
-        late = [keep.tile([P, 2, width], F32, name=f"late{c}") for c, (j0, width) in pieces]
+        late = [keep.tile([P, 2, width], F32, name=f"late{c}", tag=f"late{c}", align_bytes=ALIGN) for c, (j0, width) in pieces]
         for c, (j0, width) in pieces:
             look_up(late[c][:, 0, :], 2, j0, width)
         for c, (j0, width) in pieces:
@@ -147,7 +147,7 @@ def tile_picked_posadd_gelu_p_kernel(
                 out=h_codes[:].bitcast(FP8X4), scales=h_plane[:], in_=hidden[c][:].rearrange("p j t -> p (j t)")
             )
             if c % 2 == 0:
-                result = [keep.tile([P, 2 * width], F32, name=f"result{c}_{u}", align_bytes=ALIGN) for u in range(N // P)]
+                result = [keep.tile([P, 2 * width], F32, name=f"result{c}_{u}", tag=("late3" if (c, u) == (0, 0) else f"result{c}_{u}"), align_bytes=ALIGN) for u in range(N // P)]
             cols = slice((c % 2) * width, (c % 2 + 1) * width)
             for u in range(N // P):
                 rows = slice(u * P, (u + 1) * P)

@@ -15,6 +15,7 @@ U8 = mybir.dt.uint8
 FP8X4 = mybir.dt.float8_e4m3fn_x4
 ADD = mybir.AluOpType.add
 GELU = mybir.ActivationFunctionType.Gelu_apprx_tanh
+COPY = mybir.ActivationFunctionType.Copy
 
 P = 128
 PACK = 4
@@ -24,7 +25,8 @@ QUADS = 4
 QUAD = P // QUADS
 LIST_ROWS = 16
 ALIGN = 256
-WIDTHS = [128,128,128,128]
+WIDTH = 128
+PIECES = S // WIDTH
 
 
 def tile_picked_posadd_gelu_p_kernel(
@@ -114,42 +116,48 @@ def tile_picked_posadd_gelu_p_kernel(
                 in_=w2_scales[0, 4 * q : 4 * q + 4, :].bitcast(I32),
             )
 
-        starts = [sum(WIDTHS[:c]) for c in range(len(WIDTHS))]
-        pieces = list(enumerate(zip(starts, WIDTHS)))
-        hidden = [keep.tile([P, width, PACK], BF16, name=f"hidden{c}", align_bytes=ALIGN) for c, (j0, width) in pieces]
+        pieces = ((0, 128), (128, 128), (256, 128), (384, 128))
+        hidden = {j0: keep.tile([P, width, PACK], BF16, name=f"hidden{j0}", tag=f"hidden{j0}", align_bytes=ALIGN) for j0, width in pieces}
+        steps = ((0, 64), (64, 64), (128, 64), (192, 64), (256, 64), (320, 64), (384, 128))
+        late = {j0: keep.tile([P, 2, width], F32, name=f"late{j0}", tag=f"late{j0}", align_bytes=ALIGN) for j0, width in steps}
+
+        def entries(j0, width):
+            return offsets[:, j0 // LIST_ROWS : (j0 + width) // LIST_ROWS]
 
         def look_up(summed, t, j0, width):
-            entries = offsets[:, j0 // LIST_ROWS : (j0 + width) // LIST_ROWS]
-            nc.vector.tensor_tensor(summed, pe_table[t][:].indirect(entries), first[t][:, j0 : j0 + width], ADD)
+            nc.vector.tensor_tensor(summed, pe_table[t][:].indirect(entries(j0, width)), first[t][:, j0 : j0 + width], ADD)
 
         early = keep.tile([P, 2, S], F32, name="early")
         for t in range(2):
             look_up(early[:, t, :], t, 0, S)
-        for c, (j0, width) in pieces:
-            nc.scalar.activation(
-                hidden[c][:, :, 0:2], early[:, :, j0 : j0 + width].rearrange("p t j -> p j t"), GELU
-            )
-        late = [keep.tile([P, 2, width], F32, name=f"late{c}", tag=f"late{c}", align_bytes=ALIGN) for c, (j0, width) in pieces]
-        for c, (j0, width) in pieces:
-            look_up(late[c][:, 0, :], 2, j0, width)
-        for c, (j0, width) in pieces:
-            step = width // 2 if c == 0 else width
-            for a in range(0, width, step):
-                look_up(late[c][:, 1, a : a + step], 3, j0 + a, step)
-                nc.scalar.activation(
-                    hidden[c][:, a : a + step, 2:4], late[c][:, :, a : a + step].rearrange("p t j -> p j t"), GELU
-                )
+        for j0, width in pieces:
+            nc.scalar.activation(hidden[j0][:, :, 0:2], early[:, :, j0 : j0 + width].rearrange("p t j -> p j t"), GELU)
+        for j0, width in steps:
+            look_up(late[j0][:, 0, :], 2, j0, width)
 
-        for c, (j0, width) in pieces:
+        last_start, last_width = steps[-1]
+        fetched = keep.tile([P, last_width], F32, name="fetched")
+        nc.scalar.activation(fetched[:], pe_table[3][:].indirect(entries(last_start, last_width)), COPY)
+        for j0, width in steps:
+            if j0 < last_start:
+                look_up(late[j0][:, 1, :], 3, j0, width)
+            else:
+                nc.vector.tensor_tensor(late[j0][:, 1, :], fetched[:], first[3][:, j0:], ADD)
+            home = max(start for start, span in pieces if start <= j0)
+            nc.scalar.activation(hidden[home][:, j0 - home : j0 - home + width, 2:4], late[j0][:].rearrange("p t j -> p j t"), GELU)
+
+        stores = (((0, 128), (128, 384), (384, 512)), ((0, 256), (256, 512)))
+        result = {}
+        widths = [stores[u][0][1] for u in range(N // P)]
+        opening = keep.tile([P, sum(widths)], F32, name="opening", tag=f"late{last_start}", align_bytes=ALIGN)
+        for c, (j0, width) in enumerate(pieces):
             h_codes = keep.tile([P, width], U32, name=f"h_codes{c}", align_bytes=ALIGN)
             h_plane = keep.tile([P, width], U8, name=f"h_plane{c}", align_bytes=ALIGN)
             nc.vector.quantize_mx(
-                out=h_codes[:].bitcast(FP8X4), scales=h_plane[:], in_=hidden[c][:].rearrange("p j t -> p (j t)")
+                out=h_codes[:].bitcast(FP8X4), scales=h_plane[:], in_=hidden[j0][:].rearrange("p j t -> p (j t)")
             )
-            if c % 2 == 0:
-                result = [keep.tile([P, 2 * width], F32, name=f"result{c}_{u}", tag=("late3" if (c, u) == (0, 0) else f"result{c}_{u}"), align_bytes=ALIGN) for u in range(N // P)]
-            cols = slice((c % 2) * width, (c % 2 + 1) * width)
             for u in range(N // P):
+                lo, hi = [s for s in stores[u] if s[0] <= j0 < s[1]][0]
                 rows = slice(u * P, (u + 1) * P)
                 bank = psum.tile([P, width], F32, name=f"product{c}_{u}", tag=f"acc{(2 * c + u + PACK) % (2 * PACK)}")
                 nc.tensor.matmul_mx(
@@ -161,6 +169,10 @@ def tile_picked_posadd_gelu_p_kernel(
                     start=True,
                     stop=True,
                 )
-                (nc.scalar.copy, nc.vector.tensor_copy)[u](result[u][:, cols], bank[:])
-                if c % 2 == 1:
-                    nc.sync.dma_start(out=out[rows, j0 - width : j0 + width], in_=result[u][:])
+                if j0 == 0:
+                    result[u] = opening[:, sum(widths[:u]) : sum(widths[: u + 1])]
+                elif j0 == lo:
+                    result[u] = keep.tile([P, hi - lo], F32, name=f"result{c}_{u}", align_bytes=ALIGN)[:]
+                (nc.scalar.copy if u == 0 or c == 0 else nc.vector.tensor_copy)(result[u][:, j0 - lo : j0 - lo + width], bank[:])
+                if j0 + width == hi:
+                    nc.sync.dma_start(out=out[rows, lo:hi], in_=result[u])

@@ -51,8 +51,10 @@ def tile_picked_posadd_gelu_p_kernel(
         nc.vector.memset(xs_table[3 * QUAD : P, :].bitcast(I32), 0)
         nc.scalar.dma_start(out=xs_table[2 * QUAD : 3 * QUAD, :].bitcast(I32), in_=x_scales.bitcast(I32).rearrange("z b t -> b z t"))
 
-        w1_raw = keep.tile([P, PASSES, PACK * H], F32, name="w1_raw", tag="slot_pe2", align_bytes=ALIGN)
-        nc.sync.dma_start(out=w1_raw[:], in_=w1.rearrange("(z p j) c -> p z (j c)", z=PASSES, j=PACK))
+        w1_rows = w1.rearrange("(z p j) c -> z p (j c)", z=PASSES, j=PACK)
+        w1_raw = [keep.tile([P, PACK * H], F32, name=f"w1_raw{z}", tag=("slot_pe1", "slot_pe3")[z], align_bytes=ALIGN) for z in range(PASSES)]
+        for z in range(PASSES):
+            nc.sync.dma_start(out=w1_raw[z][:], in_=w1_rows[z])
         x_table.append(load_x(1, "slot_w2_1"))
 
         xs_picked = keep.tile([P, S], U8, name="xs_picked", align_bytes=ALIGN)
@@ -67,10 +69,10 @@ def tile_picked_posadd_gelu_p_kernel(
 
         w1_codes, w1_plane = [], []
         for z in range(PASSES):
-            grouped = keep.tile([P, PACK * H], BF16, name=f"w1_grouped{z}", tag=("slot_pe1", "slot_pe3")[z], align_bytes=ALIGN)
-            (nc.vector.tensor_copy, nc.scalar.copy)[z](
+            grouped = keep.tile([P, PACK * H], BF16, name=f"w1_grouped{z}", tag=("slot_pe2", "w1_grouped1")[z], align_bytes=ALIGN)
+            nc.vector.tensor_copy(
                 grouped[:].rearrange("p (t m j) -> p m t j", t=PACK, j=PACK),
-                w1_raw[:, z, :].rearrange("p (j m t) -> p m t j", j=PACK, t=PACK),
+                w1_raw[z][:].rearrange("p (j m t) -> p m t j", j=PACK, t=PACK),
             )
             codes = keep.tile([P, H], U32, name=f"w1_codes{z}", tag=("w1_codes0", "slot_w2_0")[z], align_bytes=ALIGN)
             plane = keep.tile([P, H], U8, name=f"w1_plane{z}", align_bytes=ALIGN)
@@ -102,9 +104,6 @@ def tile_picked_posadd_gelu_p_kernel(
                     start=(z == 0),
                     stop=(z == PASSES - 1),
                 )
-        first = [keep.tile([P, S], F32, name=f"first{t}") for t in range(PACK)]
-        for t in range(PACK):
-            nc.scalar.copy(first[t][:], acc[t][:])
 
         w2_codes = keep.tile([P, N], I32, name="w2_codes", tag="slot_w2_0", align_bytes=ALIGN)
         nc.sync.dma_start(out=w2_codes[:], in_=w2_words[0].rearrange("p n r -> p (n r)").bitcast(I32))
@@ -118,38 +117,52 @@ def tile_picked_posadd_gelu_p_kernel(
 
         pieces = ((0, 128), (128, 128), (256, 128), (384, 128))
         hidden = {j0: keep.tile([P, width, PACK], BF16, name=f"hidden{j0}", tag=f"hidden{j0}", align_bytes=ALIGN) for j0, width in pieces}
-        steps = ((0, 64), (64, 64), (128, 64), (192, 64), (256, 64), (320, 64), (384, 128))
-        late = {j0: keep.tile([P, 2, width], F32, name=f"late{j0}", tag=f"late{j0}", align_bytes=ALIGN) for j0, width in steps}
+        late = keep.tile([P, 2, S], F32, name="late", tag="late", align_bytes=ALIGN)
 
         def entries(j0, width):
             return offsets[:, j0 // LIST_ROWS : (j0 + width) // LIST_ROWS]
 
         def look_up(summed, t, j0, width):
-            nc.vector.tensor_tensor(summed, pe_table[t][:].indirect(entries(j0, width)), first[t][:, j0 : j0 + width], ADD)
+            nc.vector.tensor_tensor(summed, pe_table[t][:].indirect(entries(j0, width)), first[:, j0 : j0 + width], ADD)
 
-        early = keep.tile([P, 2, S], F32, name="early")
+        def fetch(t):
+            halves = [keep.tile([P, S // 2], F32, name=f"fetched{t}_{h}") for h in range(2)]
+            for h in range(2):
+                nc.vector.tensor_copy(halves[h][:], pe_table[t][:].indirect(entries(h * (S // 2), S // 2)))
+            return halves
+
+        early = [keep.tile([P, 2, S // 2], F32, name=f"early{h}", tag=("hold_first", "early1")[h], align_bytes=ALIGN) for h in range(2)]
         for t in range(2):
-            look_up(early[:, t, :], t, 0, S)
+            for h, half in enumerate(fetch(t)):
+                cols = slice(h * (S // 2), (h + 1) * (S // 2))
+                nc.vector.tensor_tensor(early[h][:, t, :], acc[t][:, cols], half[:], ADD)
         for j0, width in pieces:
-            nc.scalar.activation(hidden[j0][:, :, 0:2], early[:, :, j0 : j0 + width].rearrange("p t j -> p j t"), GELU)
-        for j0, width in steps:
-            look_up(late[j0][:, 0, :], 2, j0, width)
+            h, a = divmod(j0, S // 2)
+            nc.scalar.activation(hidden[j0][:, :, 0:2], early[h][:, :, a : a + width].rearrange("p t j -> p j t"), GELU)
+        first = keep.tile([P, S], F32, name="first", tag="hold_first", align_bytes=ALIGN)
+        nc.scalar.copy(first[:], acc[3][:])
+        for h, half in enumerate(fetch(2)):
+            cols = slice(h * (S // 2), (h + 1) * (S // 2))
+            nc.vector.tensor_tensor(late[:, 0, cols], acc[2][:, cols], half[:], ADD)
 
-        last_start, last_width = steps[-1]
-        fetched = keep.tile([P, last_width], F32, name="fetched")
-        nc.scalar.activation(fetched[:], pe_table[3][:].indirect(entries(last_start, last_width)), COPY)
+        by_vector = S - 192
+        steps = ((0, 64), (64, 64), (128, 64), (192, 64), (256, 64), (320, 64), (384, 128))
+        fetched = keep.tile([P, S - by_vector], F32, name="fetched")
+        nc.scalar.activation(fetched[:], pe_table[3][:].indirect(entries(by_vector, S - by_vector)), COPY)
         for j0, width in steps:
-            if j0 < last_start:
-                look_up(late[j0][:, 1, :], 3, j0, width)
-            else:
-                nc.vector.tensor_tensor(late[j0][:, 1, :], fetched[:], first[3][:, j0:], ADD)
+            if j0 < by_vector:
+                look_up(late[:, 1, j0 : j0 + width], 3, j0, width)
+            elif j0 == by_vector:
+                nc.vector.tensor_tensor(late[:, 1, j0:], fetched[:], first[:, j0:], ADD)
             home = max(start for start, span in pieces if start <= j0)
-            nc.scalar.activation(hidden[home][:, j0 - home : j0 - home + width, 2:4], late[j0][:].rearrange("p t j -> p j t"), GELU)
+            nc.scalar.activation(
+                hidden[home][:, j0 - home : j0 - home + width, 2:4], late[:, :, j0 : j0 + width].rearrange("p t j -> p j t"), GELU
+            )
 
         stores = (((0, 128), (128, 384), (384, 512)), ((0, 256), (256, 512)))
         result = {}
         widths = [stores[u][0][1] for u in range(N // P)]
-        opening = keep.tile([P, sum(widths)], F32, name="opening", tag=f"late{last_start}", align_bytes=ALIGN)
+        opening = keep.tile([P, sum(widths)], F32, name="opening", tag="late", align_bytes=ALIGN)
         for c, (j0, width) in enumerate(pieces):
             h_codes = keep.tile([P, width], U32, name=f"h_codes{c}", align_bytes=ALIGN)
             h_plane = keep.tile([P, width], U8, name=f"h_plane{c}", align_bytes=ALIGN)

@@ -123,27 +123,40 @@ def tile_picked_posadd_gelu_p_kernel(
             return offsets[:, j0 // LIST_ROWS : (j0 + width) // LIST_ROWS]
 
         def look_up(summed, t, j0, width):
-            nc.vector.tensor_tensor(summed, pe_table[t][:].indirect(entries(j0, width)), first[:, j0 : j0 + width], ADD)
+            nc.vector.tensor_tensor(summed, pe_table[t][:].indirect(entries(j0, width)), first[t][:, j0 : j0 + width], ADD)
 
-        def fetch(t):
-            halves = [keep.tile([P, S // 2], F32, name=f"fetched{t}_{h}") for h in range(2)]
-            for h in range(2):
-                nc.vector.tensor_copy(halves[h][:], pe_table[t][:].indirect(entries(h * (S // 2), S // 2)))
-            return halves
+        def fetch(t, j0, width, tag):
+            fetched = keep.tile([P, width], F32, name=f"fetched{t}_{j0}", tag=tag, align_bytes=ALIGN)
+            nc.vector.tensor_copy(fetched[:], pe_table[t][:].indirect(entries(j0, width)))
+            return fetched
 
-        early = [keep.tile([P, 2, S // 2], F32, name=f"early{h}", tag=("hold_first", "early1")[h], align_bytes=ALIGN) for h in range(2)]
-        for t in range(2):
-            for h, half in enumerate(fetch(t)):
-                cols = slice(h * (S // 2), (h + 1) * (S // 2))
-                nc.vector.tensor_tensor(early[h][:, t, :], acc[t][:, cols], half[:], ADD)
+        lead = keep.tile([P, WIDTH], F32, name="lead", tag="lead", align_bytes=ALIGN)
+        early = keep.tile([P, 2, S], F32, name="early")
+        fetched_lead = fetch(0, 0, WIDTH, "fetched_ends")
+        fetched_next = fetch(0, WIDTH, WIDTH, "fetched_next")
+        nc.vector.tensor_tensor(lead[:], acc[0][:, :WIDTH], fetched_lead[:], ADD)
+        nc.scalar.activation(hidden[0][:, :, 0], lead[:], GELU)
+        nc.vector.tensor_tensor(early[:, 0, WIDTH : 2 * WIDTH], acc[0][:, WIDTH : 2 * WIDTH], fetched_next[:], ADD)
+        fetched_rest = fetch(0, 2 * WIDTH, 2 * WIDTH, "fetched_ends")
+        nc.vector.tensor_tensor(early[:, 0, 2 * WIDTH :], acc[0][:, 2 * WIDTH :], fetched_rest[:], ADD)
+
+        fused = {1: S, 2: 384, 3: 320}
+        copied = keep.tile([P, S + 384 + 320], F32, name="copied", tag="lead", align_bytes=ALIGN)
+        first = {1: copied[:, :S], 2: copied[:, S : S + 384], 3: copied[:, S + 384 :]}
+        for t in range(1, PACK):
+            nc.scalar.copy(first[t], acc[t][:, : fused[t]])
+
         for j0, width in pieces:
-            h, a = divmod(j0, S // 2)
-            nc.scalar.activation(hidden[j0][:, :, 0:2], early[h][:, :, a : a + width].rearrange("p t j -> p j t"), GELU)
-        first = keep.tile([P, S], F32, name="first", tag="hold_first", align_bytes=ALIGN)
-        nc.scalar.copy(first[:], acc[3][:])
-        for h, half in enumerate(fetch(2)):
-            cols = slice(h * (S // 2), (h + 1) * (S // 2))
-            nc.vector.tensor_tensor(late[:, 0, cols], acc[2][:, cols], half[:], ADD)
+            look_up(early[:, 1, j0 : j0 + width], 1, j0, width)
+            if j0 == 0:
+                nc.scalar.activation(hidden[0][:, :, 1], early[:, 1, :width], GELU)
+            else:
+                nc.scalar.activation(hidden[j0][:, :, 0:2], early[:, :, j0 : j0 + width].rearrange("p t j -> p j t"), GELU)
+
+        look_up(late[:, 0, :384], 2, 0, 384)
+        fetched2 = keep.tile([P, 128], F32, name="fetched2")
+        nc.scalar.activation(fetched2[:], pe_table[2][:].indirect(entries(384, 128)), COPY)
+        nc.vector.tensor_tensor(late[:, 0, 384:], acc[2][:, 384:], fetched2[:], ADD)
 
         by_vector = S - 192
         steps = ((0, 64), (64, 64), (128, 64), (192, 64), (256, 64), (320, 64), (384, 128))
@@ -153,7 +166,7 @@ def tile_picked_posadd_gelu_p_kernel(
             if j0 < by_vector:
                 look_up(late[:, 1, j0 : j0 + width], 3, j0, width)
             elif j0 == by_vector:
-                nc.vector.tensor_tensor(late[:, 1, j0:], fetched[:], first[:, j0:], ADD)
+                nc.vector.tensor_tensor(late[:, 1, j0:], acc[3][:, j0:], fetched[:], ADD)
             home = max(start for start, span in pieces if start <= j0)
             nc.scalar.activation(
                 hidden[home][:, j0 - home : j0 - home + width, 2:4], late[:, :, j0 : j0 + width].rearrange("p t j -> p j t"), GELU

@@ -19,14 +19,16 @@ COPY = mybir.ActivationFunctionType.Copy
 
 P = 128
 PACK = 4
-K_PASS = P * PACK
-PASSES = K // K_PASS
-QUADS = 4
-QUAD = P // QUADS
+PASSES = K // (P * PACK)
+QUAD = 32
+QUAD_ORDER = (0, 2, 1, 3)
 LIST_ROWS = 16
 ALIGN = 256
-WIDTH = 128
-PIECES = S // WIDTH
+PIECE = 128
+PIECES = S // PIECE
+STEP = 64
+BY_VECTOR = {1: S, 2: 384, 3: 320}
+STORES = (((0, PIECE), (PIECE, 3 * PIECE), (3 * PIECE, S)), ((0, 2 * PIECE), (2 * PIECE, S)))
 
 
 def tile_picked_posadd_gelu_p_kernel(
@@ -49,19 +51,24 @@ def tile_picked_posadd_gelu_p_kernel(
         xs_table = keep.tile([P, T], U8, name="xs_table", tag="slot_pe0", align_bytes=ALIGN)
         nc.vector.memset(xs_table[0 : 2 * QUAD, :].bitcast(I32), 0)
         nc.vector.memset(xs_table[3 * QUAD : P, :].bitcast(I32), 0)
-        nc.scalar.dma_start(out=xs_table[2 * QUAD : 3 * QUAD, :].bitcast(I32), in_=x_scales.bitcast(I32).rearrange("z b t -> b z t"))
+        nc.scalar.dma_start(
+            out=xs_table[2 * QUAD : 3 * QUAD, :].bitcast(I32), in_=x_scales.bitcast(I32).rearrange("z b t -> b z t")
+        )
 
         w1_rows = w1.rearrange("(z p j) c -> z p (j c)", z=PASSES, j=PACK)
-        w1_raw = [keep.tile([P, PACK * H], F32, name=f"w1_raw{z}", tag=("slot_pe1", "slot_pe3")[z], align_bytes=ALIGN) for z in range(PASSES)]
+        w1_raw = [
+            keep.tile([P, PACK * H], F32, name=f"w1_raw{z}", tag=("slot_pe1", "slot_pe3")[z], align_bytes=ALIGN)
+            for z in range(PASSES)
+        ]
         for z in range(PASSES):
             nc.sync.dma_start(out=w1_raw[z][:], in_=w1_rows[z])
-        x_table.append(load_x(1, "slot_w2_1"))
+        x_table.append(load_x(1, "slot_w2_plane"))
 
         xs_picked = keep.tile([P, S], U8, name="xs_picked", align_bytes=ALIGN)
         nc.vector.tensor_copy(xs_picked[:], xs_table[:].indirect(offsets[:]))
         x_planes = keep.tile([P, PASSES, S], U8, name="x_planes", align_bytes=ALIGN)
         nc.vector.memset(x_planes[:].rearrange("p z s -> p (z s)").bitcast(I32), 0)
-        for q in (0, 2, 1, 3):
+        for q in QUAD_ORDER:
             nc.sync.dma_start(
                 out=x_planes[QUAD * q : QUAD * q + 4, :, :].bitcast(I32),
                 in_=xs_picked[2 * QUAD + 8 * q : 2 * QUAD + 8 * q + 8, :].bitcast(I32),
@@ -69,12 +76,14 @@ def tile_picked_posadd_gelu_p_kernel(
 
         w1_codes, w1_plane = [], []
         for z in range(PASSES):
-            grouped = keep.tile([P, PACK * H], BF16, name=f"w1_grouped{z}", tag=("slot_pe2", "w1_grouped1")[z], align_bytes=ALIGN)
+            grouped = keep.tile(
+                [P, PACK * H], BF16, name=f"w1_grouped{z}", tag=("slot_pe2", "w1_grouped1")[z], align_bytes=ALIGN
+            )
             nc.vector.tensor_copy(
                 grouped[:].rearrange("p (t m j) -> p m t j", t=PACK, j=PACK),
                 w1_raw[z][:].rearrange("p (j m t) -> p m t j", j=PACK, t=PACK),
             )
-            codes = keep.tile([P, H], U32, name=f"w1_codes{z}", tag=("w1_codes0", "slot_w2_0")[z], align_bytes=ALIGN)
+            codes = keep.tile([P, H], U32, name=f"w1_codes{z}", tag=("w1_codes0", "slot_w2_codes")[z], align_bytes=ALIGN)
             plane = keep.tile([P, H], U8, name=f"w1_plane{z}", align_bytes=ALIGN)
             nc.vector.quantize_mx(out=codes[:].bitcast(FP8X4), scales=plane[:], in_=grouped[:])
             w1_codes.append(codes)
@@ -87,7 +96,9 @@ def tile_picked_posadd_gelu_p_kernel(
             x_codes.append(picked)
 
         pe_rows = pe.rearrange("(p t) c -> p t c", t=PACK)
-        pe_table = [keep.tile([P, T], F32, name=f"pe_table{t}", tag=f"slot_pe{t}", align_bytes=ALIGN) for t in range(PACK)]
+        pe_table = [
+            keep.tile([P, T], F32, name=f"pe_table{t}", tag=f"slot_pe{t}", align_bytes=ALIGN) for t in range(PACK)
+        ]
         for t in range(PACK):
             nc.sync.dma_start(out=pe_table[t][:], in_=pe_rows[:, t, :])
 
@@ -105,87 +116,95 @@ def tile_picked_posadd_gelu_p_kernel(
                     stop=(z == PASSES - 1),
                 )
 
-        w2_codes = keep.tile([P, N], I32, name="w2_codes", tag="slot_w2_0", align_bytes=ALIGN)
+        w2_codes = keep.tile([P, N], I32, name="w2_codes", tag="slot_w2_codes", align_bytes=ALIGN)
         nc.sync.dma_start(out=w2_codes[:], in_=w2_words[0].rearrange("p n r -> p (n r)").bitcast(I32))
-        w2_plane = keep.tile([P, N], U8, name="w2_plane", tag="slot_w2_1", align_bytes=ALIGN)
+        w2_plane = keep.tile([P, N], U8, name="w2_plane", tag="slot_w2_plane", align_bytes=ALIGN)
         nc.vector.memset(w2_plane[:].bitcast(I32), 0)
-        for q in (0, 2, 1, 3):
+        for q in QUAD_ORDER:
             nc.sync.dma_start(
                 out=w2_plane[QUAD * q : QUAD * q + 4, :].bitcast(I32),
                 in_=w2_scales[0, 4 * q : 4 * q + 4, :].bitcast(I32),
             )
 
-        pieces = ((0, 128), (128, 128), (256, 128), (384, 128))
-        hidden = {j0: keep.tile([P, width, PACK], BF16, name=f"hidden{j0}", tag=f"hidden{j0}", align_bytes=ALIGN) for j0, width in pieces}
+        hidden = [
+            keep.tile([P, PIECE, PACK], BF16, name=f"hidden{c}", align_bytes=ALIGN) for c in range(PIECES)
+        ]
         late = keep.tile([P, 2, S], F32, name="late", tag="late", align_bytes=ALIGN)
 
-        def entries(j0, width):
-            return offsets[:, j0 // LIST_ROWS : (j0 + width) // LIST_ROWS]
+        def picked_pe(t, j0, width):
+            return pe_table[t][:].indirect(offsets[:, j0 // LIST_ROWS : (j0 + width) // LIST_ROWS])
 
-        def look_up(summed, t, j0, width):
-            nc.vector.tensor_tensor(summed, pe_table[t][:].indirect(entries(j0, width)), first[t][:, j0 : j0 + width], ADD)
+        def gather_add(summed, t, j0, width):
+            nc.vector.tensor_tensor(summed, picked_pe(t, j0, width), product[t][:, j0 : j0 + width], ADD)
 
-        def fetch(t, j0, width, tag):
-            fetched = keep.tile([P, width], F32, name=f"fetched{t}_{j0}", tag=tag, align_bytes=ALIGN)
-            nc.vector.tensor_copy(fetched[:], pe_table[t][:].indirect(entries(j0, width)))
-            return fetched
+        def gather_group0(j0, width, tag):
+            values = keep.tile([P, width], F32, name=f"group0_{j0}", tag=tag, align_bytes=ALIGN)
+            nc.vector.tensor_copy(values[:], picked_pe(0, j0, width))
+            return values
 
-        lead = keep.tile([P, WIDTH], F32, name="lead", tag="lead", align_bytes=ALIGN)
-        early = keep.tile([P, 2, S], F32, name="early")
-        fetched_lead = fetch(0, 0, WIDTH, "fetched_ends")
-        fetched_next = fetch(0, WIDTH, WIDTH, "fetched_next")
-        nc.vector.tensor_tensor(lead[:], acc[0][:, :WIDTH], fetched_lead[:], ADD)
-        nc.scalar.activation(hidden[0][:, :, 0], lead[:], GELU)
-        nc.vector.tensor_tensor(early[:, 0, WIDTH : 2 * WIDTH], acc[0][:, WIDTH : 2 * WIDTH], fetched_next[:], ADD)
-        fetched_rest = fetch(0, 2 * WIDTH, 2 * WIDTH, "fetched_ends")
-        nc.vector.tensor_tensor(early[:, 0, 2 * WIDTH :], acc[0][:, 2 * WIDTH :], fetched_rest[:], ADD)
+        def fetch_rest(t):
+            values = keep.tile([P, S - BY_VECTOR[t]], F32, name=f"rest{t}")
+            nc.scalar.activation(values[:], picked_pe(t, BY_VECTOR[t], S - BY_VECTOR[t]), COPY)
+            return values
 
-        fused = {1: S, 2: 384, 3: 320}
-        copied = keep.tile([P, S + 384 + 320], F32, name="copied", tag="lead", align_bytes=ALIGN)
-        first = {1: copied[:, :S], 2: copied[:, S : S + 384], 3: copied[:, S + 384 :]}
-        for t in range(1, PACK):
-            nc.scalar.copy(first[t], acc[t][:, : fused[t]])
-
-        for j0, width in pieces:
-            look_up(early[:, 1, j0 : j0 + width], 1, j0, width)
-            if j0 == 0:
-                nc.scalar.activation(hidden[0][:, :, 1], early[:, 1, :width], GELU)
-            else:
-                nc.scalar.activation(hidden[j0][:, :, 0:2], early[:, :, j0 : j0 + width].rearrange("p t j -> p j t"), GELU)
-
-        look_up(late[:, 0, :384], 2, 0, 384)
-        fetched2 = keep.tile([P, 128], F32, name="fetched2")
-        nc.scalar.activation(fetched2[:], pe_table[2][:].indirect(entries(384, 128)), COPY)
-        nc.vector.tensor_tensor(late[:, 0, 384:], acc[2][:, 384:], fetched2[:], ADD)
-
-        by_vector = S - 192
-        steps = ((0, 64), (64, 64), (128, 64), (192, 64), (256, 64), (320, 64), (384, 128))
-        fetched = keep.tile([P, S - by_vector], F32, name="fetched")
-        nc.scalar.activation(fetched[:], pe_table[3][:].indirect(entries(by_vector, S - by_vector)), COPY)
-        for j0, width in steps:
-            if j0 < by_vector:
-                look_up(late[:, 1, j0 : j0 + width], 3, j0, width)
-            elif j0 == by_vector:
-                nc.vector.tensor_tensor(late[:, 1, j0:], acc[3][:, j0:], fetched[:], ADD)
-            home = max(start for start, span in pieces if start <= j0)
+        def gelu_pair(sums, t, j0, width):
+            c, at = divmod(j0, PIECE)
             nc.scalar.activation(
-                hidden[home][:, j0 - home : j0 - home + width, 2:4], late[:, :, j0 : j0 + width].rearrange("p t j -> p j t"), GELU
+                hidden[c][:, at : at + width, t : t + 2], sums[:, :, j0 : j0 + width].rearrange("p t j -> p j t"), GELU
             )
 
-        stores = (((0, 128), (128, 384), (384, 512)), ((0, 256), (256, 512)))
-        result = {}
-        widths = [stores[u][0][1] for u in range(N // P)]
-        opening = keep.tile([P, sum(widths)], F32, name="opening", tag="late", align_bytes=ALIGN)
-        for c, (j0, width) in enumerate(pieces):
-            h_codes = keep.tile([P, width], U32, name=f"h_codes{c}", align_bytes=ALIGN)
-            h_plane = keep.tile([P, width], U8, name=f"h_plane{c}", align_bytes=ALIGN)
+        lead = keep.tile([P, PIECE], F32, name="lead", tag="lead", align_bytes=ALIGN)
+        early = keep.tile([P, 2, S], F32, name="early")
+        first_piece = gather_group0(0, PIECE, "group0_reused")
+        second_piece = gather_group0(PIECE, PIECE, "group0_second")
+        nc.vector.tensor_tensor(lead[:], acc[0][:, :PIECE], first_piece[:], ADD)
+        nc.scalar.activation(hidden[0][:, :, 0], lead[:], GELU)
+        nc.vector.tensor_tensor(early[:, 0, PIECE : 2 * PIECE], acc[0][:, PIECE : 2 * PIECE], second_piece[:], ADD)
+        second_half = gather_group0(2 * PIECE, 2 * PIECE, "group0_reused")
+        nc.vector.tensor_tensor(early[:, 0, 2 * PIECE :], acc[0][:, 2 * PIECE :], second_half[:], ADD)
+
+        copied = keep.tile([P, BY_VECTOR[1] + BY_VECTOR[2] + BY_VECTOR[3]], F32, name="copied", tag="lead", align_bytes=ALIGN)
+        product = {
+            1: copied[:, : BY_VECTOR[1]],
+            2: copied[:, BY_VECTOR[1] : BY_VECTOR[1] + BY_VECTOR[2]],
+            3: copied[:, BY_VECTOR[1] + BY_VECTOR[2] :],
+        }
+        for t in range(1, PACK):
+            nc.scalar.copy(product[t], acc[t][:, : BY_VECTOR[t]])
+
+        for j0 in range(0, S, PIECE):
+            gather_add(early[:, 1, j0 : j0 + PIECE], 1, j0, PIECE)
+            if j0 == 0:
+                nc.scalar.activation(hidden[0][:, :, 1], early[:, 1, :PIECE], GELU)
+            else:
+                gelu_pair(early, 0, j0, PIECE)
+
+        gather_add(late[:, 0, : BY_VECTOR[2]], 2, 0, BY_VECTOR[2])
+        rest2 = fetch_rest(2)
+        nc.vector.tensor_tensor(late[:, 0, BY_VECTOR[2] :], acc[2][:, BY_VECTOR[2] :], rest2[:], ADD)
+
+        rest3 = fetch_rest(3)
+        for j0 in range(0, BY_VECTOR[3], STEP):
+            gather_add(late[:, 1, j0 : j0 + STEP], 3, j0, STEP)
+            gelu_pair(late, 2, j0, STEP)
+        nc.vector.tensor_tensor(late[:, 1, BY_VECTOR[3] :], acc[3][:, BY_VECTOR[3] :], rest3[:], ADD)
+        gelu_pair(late, 2, BY_VECTOR[3], S - PIECE - BY_VECTOR[3])
+        gelu_pair(late, 2, S - PIECE, PIECE)
+
+        opening_widths = [ranges[0][1] for ranges in STORES]
+        opening = keep.tile([P, sum(opening_widths)], F32, name="opening", tag="late", align_bytes=ALIGN)
+        staged = [opening[:, : opening_widths[0]], opening[:, opening_widths[0] :]]
+        for c in range(PIECES):
+            j0 = c * PIECE
+            h_codes = keep.tile([P, PIECE], U32, name=f"h_codes{c}", align_bytes=ALIGN)
+            h_plane = keep.tile([P, PIECE], U8, name=f"h_plane{c}", align_bytes=ALIGN)
             nc.vector.quantize_mx(
-                out=h_codes[:].bitcast(FP8X4), scales=h_plane[:], in_=hidden[j0][:].rearrange("p j t -> p (j t)")
+                out=h_codes[:].bitcast(FP8X4), scales=h_plane[:], in_=hidden[c][:].rearrange("p j t -> p (j t)")
             )
-            for u in range(N // P):
-                lo, hi = [s for s in stores[u] if s[0] <= j0 < s[1]][0]
+            for u in (0, 1) if c < PIECES - 1 else (1, 0):
+                lo, hi = [(a, b) for a, b in STORES[u] if a <= j0 < b][0]
                 rows = slice(u * P, (u + 1) * P)
-                bank = psum.tile([P, width], F32, name=f"product{c}_{u}", tag=f"acc{(2 * c + u + PACK) % (2 * PACK)}")
+                bank = psum.tile([P, PIECE], F32, name=f"second{c}_{u}", tag=f"acc{(2 * c + u + PACK) % (2 * PACK)}")
                 nc.tensor.matmul_mx(
                     out=bank[:],
                     lhsT=w2_codes[:, rows].bitcast(FP8X4),
@@ -195,10 +214,9 @@ def tile_picked_posadd_gelu_p_kernel(
                     start=True,
                     stop=True,
                 )
-                if j0 == 0:
-                    result[u] = opening[:, sum(widths[:u]) : sum(widths[: u + 1])]
-                elif j0 == lo:
-                    result[u] = keep.tile([P, hi - lo], F32, name=f"result{c}_{u}", align_bytes=ALIGN)[:]
-                (nc.scalar.copy if u == 0 or c == 0 else nc.vector.tensor_copy)(result[u][:, j0 - lo : j0 - lo + width], bank[:])
-                if j0 + width == hi:
-                    nc.sync.dma_start(out=out[rows, lo:hi], in_=result[u])
+                if j0 == lo and lo > 0:
+                    staged[u] = keep.tile([P, hi - lo], F32, name=f"staged{c}_{u}", align_bytes=ALIGN)[:]
+                empty = nc.scalar.copy if u == 0 or c == 0 else nc.vector.tensor_copy
+                empty(staged[u][:, j0 - lo : j0 - lo + PIECE], bank[:])
+                if j0 + PIECE == hi:
+                    nc.sync.dma_start(out=out[rows, lo:hi], in_=staged[u])

@@ -1,4 +1,3 @@
-import itertools
 from contextlib import ExitStack
 
 import concourse.mybir as mybir
@@ -26,8 +25,9 @@ LIST_ROWS = 16
 ALIGN = 256
 PIECE = 128
 PIECES = S // PIECE
+HALF = S // 2
 STEP = 64
-BY_VECTOR = {1: S, 2: 384, 3: 320}
+BY_VECTOR = {0: 384, 2: 384, 3: 320}
 STORES = (((0, PIECE), (PIECE, 3 * PIECE), (3 * PIECE, S)), ((0, 2 * PIECE), (2 * PIECE, S)))
 
 
@@ -48,7 +48,7 @@ def tile_picked_posadd_gelu_p_kernel(
         offsets = keep.tile([P, S // LIST_ROWS], U16, name="offsets")
         nc.sync.dma_start(offsets[:], offs)
 
-        xs_table = keep.tile([P, T], U8, name="xs_table", tag="slot_pe0", align_bytes=ALIGN)
+        xs_table = keep.tile([P, T], U8, name="xs_table", tag="slot_pe01", align_bytes=ALIGN)
         nc.vector.memset(xs_table[0 : 2 * QUAD, :].bitcast(I32), 0)
         nc.vector.memset(xs_table[3 * QUAD : P, :].bitcast(I32), 0)
         nc.scalar.dma_start(
@@ -57,12 +57,15 @@ def tile_picked_posadd_gelu_p_kernel(
 
         w1_rows = w1.rearrange("(z p j) c -> z p (j c)", z=PASSES, j=PACK)
         w1_raw = [
-            keep.tile([P, PACK * H], F32, name=f"w1_raw{z}", tag=("slot_pe1", "slot_pe3")[z], align_bytes=ALIGN)
+            keep.tile([P, PACK * H], F32, name=f"w1_raw{z}", tag=("slot_pe2", "slot_pe3")[z], align_bytes=ALIGN)
             for z in range(PASSES)
         ]
         for z in range(PASSES):
             nc.sync.dma_start(out=w1_raw[z][:], in_=w1_rows[z])
         x_table.append(load_x(1, "slot_w2_plane"))
+
+        warm = keep.tile([P, 1], F32, name="warm")
+        nc.scalar.activation(warm[:], w1_raw[0][:, 0:1], GELU)
 
         xs_picked = keep.tile([P, S], U8, name="xs_picked", align_bytes=ALIGN)
         nc.vector.tensor_copy(xs_picked[:], xs_table[:].indirect(offsets[:]))
@@ -76,9 +79,7 @@ def tile_picked_posadd_gelu_p_kernel(
 
         w1_codes, w1_plane = [], []
         for z in range(PASSES):
-            grouped = keep.tile(
-                [P, PACK * H], BF16, name=f"w1_grouped{z}", tag=("slot_pe2", "w1_grouped1")[z], align_bytes=ALIGN
-            )
+            grouped = keep.tile([P, PACK * H], BF16, name=f"w1_grouped{z}", align_bytes=ALIGN)
             nc.vector.tensor_copy(
                 grouped[:].rearrange("p (t m j) -> p m t j", t=PACK, j=PACK),
                 w1_raw[z][:].rearrange("p (j m t) -> p m t j", j=PACK, t=PACK),
@@ -96,25 +97,26 @@ def tile_picked_posadd_gelu_p_kernel(
             x_codes.append(picked)
 
         pe_rows = pe.rearrange("(p t) c -> p t c", t=PACK)
-        pe_table = [
-            keep.tile([P, T], F32, name=f"pe_table{t}", tag=f"slot_pe{t}", align_bytes=ALIGN) for t in range(PACK)
-        ]
-        for t in range(PACK):
-            nc.sync.dma_start(out=pe_table[t][:], in_=pe_rows[:, t, :])
+        pe01 = keep.tile([P, 2 * T], F32, name="pe01", tag="slot_pe01", align_bytes=ALIGN)
+        nc.sync.dma_start(out=pe01[:], in_=pe.rearrange("(p h t) c -> p h (t c)", h=2, t=2)[:, 0, :])
+        window = {0: pe01[:], 1: pe01[:, T:]}
+        for t in (2, 3):
+            table = keep.tile([P, T], F32, name=f"pe_table{t}", tag=f"slot_pe{t}", align_bytes=ALIGN)
+            nc.sync.dma_start(out=table[:], in_=pe_rows[:, t, :])
+            window[t] = table[:]
 
         acc = [psum.tile([P, S], F32, name=f"acc{t}", tag=f"acc{t}") for t in range(PACK)]
-        for pair in range(0, PACK, 2):
-            for z, t in itertools.product(range(PASSES), (pair, pair + 1)):
-                cols = slice(t * P, (t + 1) * P)
-                nc.tensor.matmul_mx(
-                    out=acc[t][:],
-                    lhsT=w1_codes[z][:, cols].bitcast(FP8X4),
-                    lhsT_scale=w1_plane[z][:, cols],
-                    rhs=x_codes[z][:].bitcast(FP8X4),
-                    rhs_scale=x_planes[:, z, :],
-                    start=(z == 0),
-                    stop=(z == PASSES - 1),
-                )
+        for z, t in ((0, 0), (0, 2), (1, 0), (1, 2), (0, 3), (1, 3), (0, 1), (1, 1)):
+            cols = slice(t * P, (t + 1) * P)
+            nc.tensor.matmul_mx(
+                out=acc[t][:],
+                lhsT=w1_codes[z][:, cols].bitcast(FP8X4),
+                lhsT_scale=w1_plane[z][:, cols],
+                rhs=x_codes[z][:].bitcast(FP8X4),
+                rhs_scale=x_planes[:, z, :],
+                start=(z == 0),
+                stop=(z == PASSES - 1),
+            )
 
         w2_codes = keep.tile([P, N], I32, name="w2_codes", tag="slot_w2_codes", align_bytes=ALIGN)
         nc.sync.dma_start(out=w2_codes[:], in_=w2_words[0].rearrange("p n r -> p (n r)").bitcast(I32))
@@ -126,70 +128,56 @@ def tile_picked_posadd_gelu_p_kernel(
                 in_=w2_scales[0, 4 * q : 4 * q + 4, :].bitcast(I32),
             )
 
-        hidden = [
-            keep.tile([P, PIECE, PACK], BF16, name=f"hidden{c}", align_bytes=ALIGN) for c in range(PIECES)
-        ]
+        hidden = [keep.tile([P, PIECE, PACK], BF16, name=f"hidden{c}", align_bytes=ALIGN)[:] for c in range(2)]
+        early = keep.tile([P, 2, S], F32, name="early")
         late = keep.tile([P, 2, S], F32, name="late", tag="late", align_bytes=ALIGN)
 
         def picked_pe(t, j0, width):
-            return pe_table[t][:].indirect(offsets[:, j0 // LIST_ROWS : (j0 + width) // LIST_ROWS])
+            return window[t].indirect(offsets[:, j0 // LIST_ROWS : (j0 + width) // LIST_ROWS])
 
         def gather_add(summed, t, j0, width):
             nc.vector.tensor_tensor(summed, picked_pe(t, j0, width), product[t][:, j0 : j0 + width], ADD)
 
-        def gather_group0(j0, width, tag):
-            values = keep.tile([P, width], F32, name=f"group0_{j0}", tag=tag, align_bytes=ALIGN)
-            nc.vector.tensor_copy(values[:], picked_pe(0, j0, width))
-            return values
-
-        def fetch_rest(t):
-            values = keep.tile([P, S - BY_VECTOR[t]], F32, name=f"rest{t}")
-            nc.scalar.activation(values[:], picked_pe(t, BY_VECTOR[t], S - BY_VECTOR[t]), COPY)
+        def fetch(t, j0, width):
+            values = keep.tile([P, width], F32, name=f"fetched{t}_{j0}")
+            nc.scalar.activation(values[:], picked_pe(t, j0, width), COPY)
             return values
 
         def gelu_pair(sums, t, j0, width):
             c, at = divmod(j0, PIECE)
-            nc.scalar.activation(
-                hidden[c][:, at : at + width, t : t + 2], sums[:, :, j0 : j0 + width].rearrange("p t j -> p j t"), GELU
-            )
+            nc.scalar.activation(hidden[c][:, at : at + width, t : t + 2], sums.rearrange("p t j -> p j t"), GELU)
 
-        lead = keep.tile([P, PIECE], F32, name="lead", tag="lead", align_bytes=ALIGN)
-        early = keep.tile([P, 2, S], F32, name="early")
-        first_piece = gather_group0(0, PIECE, "group0_reused")
-        second_piece = gather_group0(PIECE, PIECE, "group0_second")
-        nc.vector.tensor_tensor(lead[:], acc[0][:, :PIECE], first_piece[:], ADD)
-        nc.scalar.activation(hidden[0][:, :, 0], lead[:], GELU)
-        nc.vector.tensor_tensor(early[:, 0, PIECE : 2 * PIECE], acc[0][:, PIECE : 2 * PIECE], second_piece[:], ADD)
-        second_half = gather_group0(2 * PIECE, 2 * PIECE, "group0_reused")
-        nc.vector.tensor_tensor(early[:, 0, 2 * PIECE :], acc[0][:, 2 * PIECE :], second_half[:], ADD)
+        product = {t: keep.tile([P, BY_VECTOR[t]], F32, name=f"product{t}") for t in BY_VECTOR}
+        opener = keep.tile([P, PIECE], F32, name="opener", tag="opener", align_bytes=ALIGN)
+        nc.vector.tensor_copy(product[0][:], acc[0][:, : BY_VECTOR[0]])
+        nc.vector.tensor_copy(opener[:], acc[2][:, :PIECE])
+        nc.vector.tensor_copy(product[2][:, PIECE:], acc[2][:, PIECE : BY_VECTOR[2]])
+        nc.vector.tensor_copy(product[3][:], acc[3][:, : BY_VECTOR[3]])
 
-        copied = keep.tile([P, BY_VECTOR[1] + BY_VECTOR[2] + BY_VECTOR[3]], F32, name="copied", tag="lead", align_bytes=ALIGN)
-        product = {
-            1: copied[:, : BY_VECTOR[1]],
-            2: copied[:, BY_VECTOR[1] : BY_VECTOR[1] + BY_VECTOR[2]],
-            3: copied[:, BY_VECTOR[1] + BY_VECTOR[2] :],
-        }
-        for t in range(1, PACK):
-            nc.scalar.copy(product[t], acc[t][:, : BY_VECTOR[t]])
+        shares = ((1, 0, HALF), (1, HALF, HALF), (0, BY_VECTOR[0], S - BY_VECTOR[0]))
+        fetched = [fetch(t, j0, width) for t, j0, width in shares]
+        gather_add(early[:, 0, : BY_VECTOR[0]], 0, 0, BY_VECTOR[0])
+        for (t, j0, width), values in zip(shares, fetched):
+            nc.vector.tensor_tensor(early[:, t, j0 : j0 + width], acc[t][:, j0 : j0 + width], values[:], ADD)
+        for j0 in range(0, HALF, PIECE):
+            gelu_pair(early[:, :, j0 : j0 + PIECE], 0, j0, PIECE)
 
-        for j0 in range(0, S, PIECE):
-            gather_add(early[:, 1, j0 : j0 + PIECE], 1, j0, PIECE)
-            if j0 == 0:
-                nc.scalar.activation(hidden[0][:, :, 1], early[:, 1, :PIECE], GELU)
-            else:
-                gelu_pair(early, 0, j0, PIECE)
-
-        gather_add(late[:, 0, : BY_VECTOR[2]], 2, 0, BY_VECTOR[2])
-        rest2 = fetch_rest(2)
+        nc.vector.tensor_tensor(late[:, 0, :PIECE], picked_pe(2, 0, PIECE), opener[:], ADD)
+        gather_add(late[:, 0, PIECE : BY_VECTOR[2]], 2, PIECE, BY_VECTOR[2] - PIECE)
+        rest2 = fetch(2, BY_VECTOR[2], S - BY_VECTOR[2])
         nc.vector.tensor_tensor(late[:, 0, BY_VECTOR[2] :], acc[2][:, BY_VECTOR[2] :], rest2[:], ADD)
+        second_half = keep.tile([P, HALF, PACK], BF16, name="hidden_second_half", tag="opener", align_bytes=ALIGN)
+        hidden.extend([second_half[:, :PIECE, :], second_half[:, PIECE:, :]])
+        for j0 in range(HALF, S, PIECE):
+            gelu_pair(early[:, :, j0 : j0 + PIECE], 0, j0, PIECE)
 
-        rest3 = fetch_rest(3)
+        rest3 = fetch(3, BY_VECTOR[3], S - BY_VECTOR[3])
         for j0 in range(0, BY_VECTOR[3], STEP):
             gather_add(late[:, 1, j0 : j0 + STEP], 3, j0, STEP)
-            gelu_pair(late, 2, j0, STEP)
+            gelu_pair(late[:, :, j0 : j0 + STEP], 2, j0, STEP)
         nc.vector.tensor_tensor(late[:, 1, BY_VECTOR[3] :], acc[3][:, BY_VECTOR[3] :], rest3[:], ADD)
-        gelu_pair(late, 2, BY_VECTOR[3], S - PIECE - BY_VECTOR[3])
-        gelu_pair(late, 2, S - PIECE, PIECE)
+        gelu_pair(late[:, :, BY_VECTOR[3] : S - PIECE], 2, BY_VECTOR[3], S - PIECE - BY_VECTOR[3])
+        gelu_pair(late[:, :, S - PIECE :], 2, S - PIECE, PIECE)
 
         opening_widths = [ranges[0][1] for ranges in STORES]
         opening = keep.tile([P, sum(opening_widths)], F32, name="opening", tag="late", align_bytes=ALIGN)
@@ -199,7 +187,7 @@ def tile_picked_posadd_gelu_p_kernel(
             h_codes = keep.tile([P, PIECE], U32, name=f"h_codes{c}", align_bytes=ALIGN)
             h_plane = keep.tile([P, PIECE], U8, name=f"h_plane{c}", align_bytes=ALIGN)
             nc.vector.quantize_mx(
-                out=h_codes[:].bitcast(FP8X4), scales=h_plane[:], in_=hidden[c][:].rearrange("p j t -> p (j t)")
+                out=h_codes[:].bitcast(FP8X4), scales=h_plane[:], in_=hidden[c].rearrange("p j t -> p (j t)")
             )
             for u in (0, 1) if c < PIECES - 1 else (1, 0):
                 lo, hi = [(a, b) for a, b in STORES[u] if a <= j0 < b][0]

@@ -64,8 +64,10 @@ def tile_picked_posadd_gelu_p_kernel(
             nc.sync.dma_start(out=w1_raw[z][:], in_=w1_rows[z])
         x_table.append(load_x(1, "slot_w2_plane"))
 
+        zero = keep.tile([P, 1], F32, name="zero")
+        nc.vector.memset(zero[:], 0.0)
         warm = keep.tile([P, 1], F32, name="warm")
-        nc.scalar.activation(warm[:], w1_raw[0][:, 0:1], GELU)
+        nc.scalar.activation(warm[:], zero[:], GELU)
 
         xs_picked = keep.tile([P, S], U8, name="xs_picked", align_bytes=ALIGN)
         nc.vector.tensor_copy(xs_picked[:], xs_table[:].indirect(offsets[:]))
@@ -207,4 +209,5 @@ def tile_picked_posadd_gelu_p_kernel(
                 empty = nc.scalar.copy if u == 0 or c == 0 else nc.vector.tensor_copy
                 empty(staged[u][:, j0 - lo : j0 - lo + PIECE], bank[:])
                 if j0 + PIECE == hi:
-                    nc.sync.dma_start(out=out[rows, lo:hi], in_=staged[u])
+                    queue = nc.scalar if u == 0 and hi == S else nc.sync
+                    queue.dma_start(out=out[rows, lo:hi], in_=staged[u])

@@ -209,5 +209,4 @@ def tile_picked_posadd_gelu_p_kernel(
                 empty = nc.scalar.copy if u == 0 or c == 0 else nc.vector.tensor_copy
                 empty(staged[u][:, j0 - lo : j0 - lo + PIECE], bank[:])
                 if j0 + PIECE == hi:
-                    queue = nc.scalar if u == 0 and hi == S else nc.sync
-                    queue.dma_start(out=out[rows, lo:hi], in_=staged[u])
+                    nc.sync.dma_start(out=out[rows, lo:hi], in_=staged[u])

@@ -121,7 +121,9 @@ def tile_picked_posadd_gelu_p_kernel(
             )
 
         w2_codes = keep.tile([P, N], I32, name="w2_codes", tag="slot_w2_codes", align_bytes=ALIGN)
-        nc.sync.dma_start(out=w2_codes[:], in_=w2_words[0].rearrange("p n r -> p (n r)").bitcast(I32))
+        w2_rows = w2_words[0].rearrange("p n r -> p (n r)").bitcast(I32)
+        nc.sync.dma_start(out=w2_codes[:, :STEP], in_=w2_rows[:, :STEP])
+        nc.sync.dma_start(out=w2_codes[:, STEP:], in_=w2_rows[:, STEP:])
         w2_plane = keep.tile([P, N], U8, name="w2_plane", tag="slot_w2_plane", align_bytes=ALIGN)
         nc.vector.memset(w2_plane[:].bitcast(I32), 0)
         for q in QUAD_ORDER:

@@ -44,11 +44,11 @@ def tile_picked_posadd_gelu_p_kernel(
             nc.sync.dma_start(out=table[:], in_=x_words[z].rearrange("p n r -> p (n r)").bitcast(I32))
             return table
 
-        x_table = [load_x(0, "x_table0")]
+        x_table = [load_x(0, "slot_pe01")]
         offsets = keep.tile([P, S // LIST_ROWS], U16, name="offsets")
         nc.sync.dma_start(offsets[:], offs)
 
-        xs_table = keep.tile([P, T], U8, name="xs_table", tag="slot_pe01", align_bytes=ALIGN)
+        xs_table = keep.tile([P, T], U8, name="xs_table", tag="slot_w2_plane", align_bytes=ALIGN)
         nc.vector.memset(xs_table[0 : 2 * QUAD, :].bitcast(I32), 0)
         nc.vector.memset(xs_table[3 * QUAD : P, :].bitcast(I32), 0)
         nc.scalar.dma_start(
@@ -62,7 +62,6 @@ def tile_picked_posadd_gelu_p_kernel(
         ]
         for z in range(PASSES):
             nc.sync.dma_start(out=w1_raw[z][:], in_=w1_rows[z])
-        x_table.append(load_x(1, "slot_w2_plane"))
 
         zero = keep.tile([P, 1], F32, name="zero")
         nc.vector.memset(zero[:], 0.0)
@@ -73,11 +72,18 @@ def tile_picked_posadd_gelu_p_kernel(
         nc.vector.tensor_copy(xs_picked[:], xs_table[:].indirect(offsets[:]))
         x_planes = keep.tile([P, PASSES, S], U8, name="x_planes", align_bytes=ALIGN)
         nc.vector.memset(x_planes[:].rearrange("p z s -> p (z s)").bitcast(I32), 0)
-        for q in QUAD_ORDER:
+
+        def move_scales(q):
             nc.sync.dma_start(
                 out=x_planes[QUAD * q : QUAD * q + 4, :, :].bitcast(I32),
                 in_=xs_picked[2 * QUAD + 8 * q : 2 * QUAD + 8 * q + 8, :].bitcast(I32),
             )
+
+        for q in QUAD_ORDER[:2]:
+            move_scales(q)
+        x_table.append(load_x(1, "slot_w2_plane"))
+        for q in QUAD_ORDER[2:]:
+            move_scales(q)
 
         w1_codes, w1_plane = [], []
         for z in range(PASSES):

from contextlib import ExitStack

import concourse.mybir as mybir

K, T, S, H, N = 1024, 2048, 512, 512, 256
FLOPS = 2 * K * H * S + 2 * H * N * S

F32 = mybir.dt.float32
BF16 = mybir.dt.bfloat16
I32 = mybir.dt.int32
U32 = mybir.dt.uint32
U16 = mybir.dt.uint16
U8 = mybir.dt.uint8
FP8X4 = mybir.dt.float8_e4m3fn_x4
ADD = mybir.AluOpType.add
GELU = mybir.ActivationFunctionType.Gelu_apprx_tanh
COPY = mybir.ActivationFunctionType.Copy

P = 128
PACK = 4
PASSES = K // (P * PACK)
QUAD = 32
QUAD_ORDER = (0, 2, 1, 3)
LIST_ROWS = 16
ALIGN = 256
PIECE = 128
PIECES = S // PIECE
HALF = S // 2
STEP = 64
BY_VECTOR = {0: 384, 2: 384, 3: 320}
STORES = (((0, PIECE), (PIECE, 3 * PIECE), (3 * PIECE, S)), ((0, 2 * PIECE), (2 * PIECE, S)))


def tile_picked_posadd_gelu_p_kernel(
    tc, x_words, x_scales, w1, w2_words, w2_scales, pe, offs, out
):
    nc = tc.nc
    with ExitStack() as ctx:
        keep = ctx.enter_context(tc.tile_pool(name="keep", bufs=1))
        psum = ctx.enter_context(tc.psum_pool(name="psum", bufs=1))

        def load_x(z, tag):
            table = keep.tile([P, T], I32, name=f"x_table{z}", tag=tag, align_bytes=ALIGN)
            nc.sync.dma_start(out=table[:], in_=x_words[z].rearrange("p n r -> p (n r)").bitcast(I32))
            return table

        x_table = [load_x(0, "slot_pe01")]
        offsets = keep.tile([P, S // LIST_ROWS], U16, name="offsets")
        nc.sync.dma_start(offsets[:], offs)

        xs_table = keep.tile([P, T], U8, name="xs_table", tag="slot_w2_plane", align_bytes=ALIGN)
        nc.vector.memset(xs_table[0 : 2 * QUAD, :].bitcast(I32), 0)
        nc.vector.memset(xs_table[3 * QUAD : P, :].bitcast(I32), 0)
        nc.scalar.dma_start(
            out=xs_table[2 * QUAD : 3 * QUAD, :].bitcast(I32), in_=x_scales.bitcast(I32).rearrange("z b t -> b z t")
        )

        w1_rows = w1.rearrange("(z p j) c -> z p (j c)", z=PASSES, j=PACK)
        w1_raw = [
            keep.tile([P, PACK * H], F32, name=f"w1_raw{z}", tag=("slot_pe2", "slot_pe3")[z], align_bytes=ALIGN)
            for z in range(PASSES)
        ]
        for z in range(PASSES):
            nc.sync.dma_start(out=w1_raw[z][:], in_=w1_rows[z])

        zero = keep.tile([P, 1], F32, name="zero")
        nc.vector.memset(zero[:], 0.0)
        warm = keep.tile([P, 1], F32, name="warm")
        nc.scalar.activation(warm[:], zero[:], GELU)

        xs_picked = keep.tile([P, S], U8, name="xs_picked", align_bytes=ALIGN)
        nc.vector.tensor_copy(xs_picked[:], xs_table[:].indirect(offsets[:]))
        x_planes = keep.tile([P, PASSES, S], U8, name="x_planes", align_bytes=ALIGN)
        nc.vector.memset(x_planes[:].rearrange("p z s -> p (z s)").bitcast(I32), 0)

        def move_scales(q):
            nc.sync.dma_start(
                out=x_planes[QUAD * q : QUAD * q + 4, :, :].bitcast(I32),
                in_=xs_picked[2 * QUAD + 8 * q : 2 * QUAD + 8 * q + 8, :].bitcast(I32),
            )

        for q in QUAD_ORDER[:2]:
            move_scales(q)
        x_table.append(load_x(1, "slot_w2_plane"))
        for q in QUAD_ORDER[2:]:
            move_scales(q)

        w1_codes, w1_plane = [], []
        for z in range(PASSES):
            grouped = keep.tile([P, PACK * H], BF16, name=f"w1_grouped{z}", align_bytes=ALIGN)
            nc.vector.tensor_copy(
                grouped[:].rearrange("p (t m j) -> p m t j", t=PACK, j=PACK),
                w1_raw[z][:].rearrange("p (j m t) -> p m t j", j=PACK, t=PACK),
            )
            codes = keep.tile([P, H], U32, name=f"w1_codes{z}", tag=("w1_codes0", "slot_w2_codes")[z], align_bytes=ALIGN)
            plane = keep.tile([P, H], U8, name=f"w1_plane{z}", align_bytes=ALIGN)
            nc.vector.quantize_mx(out=codes[:].bitcast(FP8X4), scales=plane[:], in_=grouped[:])
            w1_codes.append(codes)
            w1_plane.append(plane)

        x_codes = []
        for z in range(PASSES):
            picked = keep.tile([P, S], U32, name=f"x_codes{z}", align_bytes=ALIGN)
            nc.vector.tensor_copy(picked[:], x_table[z][:].bitcast(U32).indirect(offsets[:]))
            x_codes.append(picked)

        pe_rows = pe.rearrange("(p t) c -> p t c", t=PACK)
        pe01 = keep.tile([P, 2 * T], F32, name="pe01", tag="slot_pe01", align_bytes=ALIGN)
        nc.sync.dma_start(out=pe01[:], in_=pe.rearrange("(p h t) c -> p h (t c)", h=2, t=2)[:, 0, :])
        window = {0: pe01[:], 1: pe01[:, T:]}
        for t in (2, 3):
            table = keep.tile([P, T], F32, name=f"pe_table{t}", tag=f"slot_pe{t}", align_bytes=ALIGN)
            nc.sync.dma_start(out=table[:], in_=pe_rows[:, t, :])
            window[t] = table[:]

        acc = [psum.tile([P, S], F32, name=f"acc{t}", tag=f"acc{t}") for t in range(PACK)]
        for z, t in ((0, 0), (0, 2), (1, 0), (1, 2), (0, 3), (1, 3), (0, 1), (1, 1)):
            cols = slice(t * P, (t + 1) * P)
            nc.tensor.matmul_mx(
                out=acc[t][:],
                lhsT=w1_codes[z][:, cols].bitcast(FP8X4),
                lhsT_scale=w1_plane[z][:, cols],
                rhs=x_codes[z][:].bitcast(FP8X4),
                rhs_scale=x_planes[:, z, :],
                start=(z == 0),
                stop=(z == PASSES - 1),
            )

        w2_codes = keep.tile([P, N], I32, name="w2_codes", tag="slot_w2_codes", align_bytes=ALIGN)
        w2_rows = w2_words[0].rearrange("p n r -> p (n r)").bitcast(I32)
        nc.sync.dma_start(out=w2_codes[:, :STEP], in_=w2_rows[:, :STEP])
        nc.sync.dma_start(out=w2_codes[:, STEP:], in_=w2_rows[:, STEP:])
        w2_plane = keep.tile([P, N], U8, name="w2_plane", tag="slot_w2_plane", align_bytes=ALIGN)
        nc.vector.memset(w2_plane[:].bitcast(I32), 0)
        for q in QUAD_ORDER:
            nc.sync.dma_start(
                out=w2_plane[QUAD * q : QUAD * q + 4, :].bitcast(I32),
                in_=w2_scales[0, 4 * q : 4 * q + 4, :].bitcast(I32),
            )

        hidden = [keep.tile([P, PIECE, PACK], BF16, name=f"hidden{c}", align_bytes=ALIGN)[:] for c in range(2)]
        early = keep.tile([P, 2, S], F32, name="early")
        late = keep.tile([P, 2, S], F32, name="late", tag="late", align_bytes=ALIGN)

        def picked_pe(t, j0, width):
            return window[t].indirect(offsets[:, j0 // LIST_ROWS : (j0 + width) // LIST_ROWS])

        def gather_add(summed, t, j0, width):
            nc.vector.tensor_tensor(summed, picked_pe(t, j0, width), product[t][:, j0 : j0 + width], ADD)

        def fetch(t, j0, width):
            values = keep.tile([P, width], F32, name=f"fetched{t}_{j0}")
            nc.scalar.activation(values[:], picked_pe(t, j0, width), COPY)
            return values

        def gelu_pair(sums, t, j0, width):
            c, at = divmod(j0, PIECE)
            nc.scalar.activation(hidden[c][:, at : at + width, t : t + 2], sums.rearrange("p t j -> p j t"), GELU)

        product = {t: keep.tile([P, BY_VECTOR[t]], F32, name=f"product{t}") for t in BY_VECTOR}
        opener = keep.tile([P, PIECE], F32, name="opener", tag="opener", align_bytes=ALIGN)
        nc.vector.tensor_copy(product[0][:], acc[0][:, : BY_VECTOR[0]])
        nc.vector.tensor_copy(opener[:], acc[2][:, :PIECE])
        nc.vector.tensor_copy(product[2][:, PIECE:], acc[2][:, PIECE : BY_VECTOR[2]])
        nc.vector.tensor_copy(product[3][:], acc[3][:, : BY_VECTOR[3]])

        shares = ((1, 0, HALF), (1, HALF, HALF), (0, BY_VECTOR[0], S - BY_VECTOR[0]))
        fetched = [fetch(t, j0, width) for t, j0, width in shares]
        gather_add(early[:, 0, : BY_VECTOR[0]], 0, 0, BY_VECTOR[0])
        for (t, j0, width), values in zip(shares, fetched):
            nc.vector.tensor_tensor(early[:, t, j0 : j0 + width], acc[t][:, j0 : j0 + width], values[:], ADD)
        for j0 in range(0, HALF, PIECE):
            gelu_pair(early[:, :, j0 : j0 + PIECE], 0, j0, PIECE)

        nc.vector.tensor_tensor(late[:, 0, :PIECE], picked_pe(2, 0, PIECE), opener[:], ADD)
        gather_add(late[:, 0, PIECE : BY_VECTOR[2]], 2, PIECE, BY_VECTOR[2] - PIECE)
        rest2 = fetch(2, BY_VECTOR[2], S - BY_VECTOR[2])
        nc.vector.tensor_tensor(late[:, 0, BY_VECTOR[2] :], acc[2][:, BY_VECTOR[2] :], rest2[:], ADD)
        second_half = keep.tile([P, HALF, PACK], BF16, name="hidden_second_half", tag="opener", align_bytes=ALIGN)
        hidden.extend([second_half[:, :PIECE, :], second_half[:, PIECE:, :]])
        for j0 in range(HALF, S, PIECE):
            gelu_pair(early[:, :, j0 : j0 + PIECE], 0, j0, PIECE)

        rest3 = fetch(3, BY_VECTOR[3], S - BY_VECTOR[3])
        for j0 in range(0, BY_VECTOR[3], STEP):
            gather_add(late[:, 1, j0 : j0 + STEP], 3, j0, STEP)
            gelu_pair(late[:, :, j0 : j0 + STEP], 2, j0, STEP)
        nc.vector.tensor_tensor(late[:, 1, BY_VECTOR[3] :], acc[3][:, BY_VECTOR[3] :], rest3[:], ADD)
        gelu_pair(late[:, :, BY_VECTOR[3] : S - PIECE], 2, BY_VECTOR[3], S - PIECE - BY_VECTOR[3])
        gelu_pair(late[:, :, S - PIECE :], 2, S - PIECE, PIECE)

        opening_widths = [ranges[0][1] for ranges in STORES]
        opening = keep.tile([P, sum(opening_widths)], F32, name="opening", tag="late", align_bytes=ALIGN)
        staged = [opening[:, : opening_widths[0]], opening[:, opening_widths[0] :]]
        for c in range(PIECES):
            j0 = c * PIECE
            h_codes = keep.tile([P, PIECE], U32, name=f"h_codes{c}", align_bytes=ALIGN)
            h_plane = keep.tile([P, PIECE], U8, name=f"h_plane{c}", align_bytes=ALIGN)
            nc.vector.quantize_mx(
                out=h_codes[:].bitcast(FP8X4), scales=h_plane[:], in_=hidden[c].rearrange("p j t -> p (j t)")
            )
            for u in (0, 1) if c < PIECES - 1 else (1, 0):
                lo, hi = [(a, b) for a, b in STORES[u] if a <= j0 < b][0]
                rows = slice(u * P, (u + 1) * P)
                bank = psum.tile([P, PIECE], F32, name=f"second{c}_{u}", tag=f"acc{(2 * c + u + PACK) % (2 * PACK)}")
                nc.tensor.matmul_mx(
                    out=bank[:],
                    lhsT=w2_codes[:, rows].bitcast(FP8X4),
                    lhsT_scale=w2_plane[:, rows],
                    rhs=h_codes[:].bitcast(FP8X4),
                    rhs_scale=h_plane[:],
                    start=True,
                    stop=True,
                )
                if j0 == lo and lo > 0:
                    staged[u] = keep.tile([P, hi - lo], F32, name=f"staged{c}_{u}", align_bytes=ALIGN)[:]
                empty = nc.scalar.copy if u == 0 or c == 0 else nc.vector.tensor_copy
                empty(staged[u][:, j0 - lo : j0 - lo + PIECE], bank[:])
                if j0 + PIECE == hi:
                    nc.sync.dma_start(out=out[rows, lo:hi], in_=staged[u])
